import numpy as np
import ml_dtypes


def mxq(x, axis, fmt="e4m3"):
    dtype, down = {"e4m3": (ml_dtypes.float8_e4m3fn, 7), "e5m2": (ml_dtypes.float8_e5m2, 14)}[fmt]
    v = np.moveaxis(np.asarray(x, np.float32).astype(ml_dtypes.bfloat16).astype(np.float64), axis, -1)
    blocks = v.reshape(v.shape[:-1] + (-1, 32))
    amax = np.abs(blocks).max(-1, keepdims=True)
    byte = np.maximum(np.where(amax > 0, np.frexp(amax)[1] - 1 + 127, 0) - down, 1)
    scale = np.exp2(byte - 127.0)
    codes = (blocks / scale).astype(np.float32).astype(dtype).astype(np.float64)
    return np.moveaxis((codes * scale).reshape(v.shape), -1, axis)


WIDE = False


def mx_kscale(k):
    if not WIDE:
        return np.ones(k)
    levels = np.array([10, -10, 5, -5, 0])
    if k % 512:
        return np.exp2(np.random.permutation(np.resize(levels, k // 32))).repeat(32)
    a = np.empty((k // 512, 16))
    for p in range(k // 512):
        a[p, :8] = np.random.permutation(np.resize(levels, 8))
        for g in range(8):
            far = levels[np.abs(levels - a[p, g]) >= 10]
            a[p, g + 8] = far[np.random.randint(len(far))]
    return np.exp2(a.ravel()).repeat(32)


def f64(x):
    return np.asarray(x).astype(np.float64)


def striped(idx):
    return np.tile(idx.reshape(-1, 16).T, (8, 1)).astype(np.uint16)


def unstriped(offs):
    return offs[:16].T.reshape(-1).astype(np.int64)


def striped8(idx):
    return np.concatenate([x.reshape(-1, 16).T for x in idx]).astype(np.uint16)


def runs(offs, k):
    lists = np.stack([offs[16 * r : 16 * r + 16].T.reshape(-1) for r in range(8)]).astype(np.int64)
    return lists[np.arange(k) % 512 // 64]


def pack_weight(w):
    k, n = w.shape
    w = f64(np.asarray(w, np.float32).astype(ml_dtypes.bfloat16)).reshape(k // 32, 32, n)
    amax = np.abs(w).max(1)
    byte = np.clip(np.where(amax > 0, np.frexp(amax)[1] - 1 + 127 - 7, 1), 1, 254)
    scaled = (w * np.exp2(127.0 - byte)[:, None, :]).reshape(k, n).astype(np.float32)
    words = np.ascontiguousarray(scaled.reshape(k // 512, 128, 4, n).transpose(0, 1, 3, 2)).astype(ml_dtypes.float8_e4m3fn).view(np.uint8)
    return words, np.ascontiguousarray(byte.astype(np.uint8).reshape(k // 512, 16, n))


def unpack_weight(words, scales):
    g, p, n, _ = words.shape
    vals = np.ascontiguousarray(words).view(ml_dtypes.float8_e4m3fn).astype(np.float64) * np.repeat(np.exp2(scales.astype(np.float64) - 127.0), 8, axis=1)[..., None]
    return vals.transpose(0, 1, 3, 2).reshape(g * 512, n)


def relu(v):
    return np.maximum(v, 0.0)

def planes(y):
    n, m = y.shape
    v = y.astype(np.float32).astype(ml_dtypes.bfloat16).astype(np.float64).reshape(n // 32, 32, m)
    top = np.abs(v).max(1)
    byte = np.clip(np.where(top > 0, np.frexp(top)[1] - 1 + 127 - 7, 1), 1, 254)
    codes = (v * np.exp2(127.0 - byte)[:, None, :]).reshape(n, m).astype(np.float32).astype(ml_dtypes.float8_e4m3fn).view(np.uint8)
    words = codes.reshape(n // 512, 128, 4, m).transpose(0, 1, 3, 2)
    return np.ascontiguousarray(words), np.ascontiguousarray(byte.astype(np.uint8).reshape(n // 512, 16, m))


K, T, S, N = 512, 2048, 512, 512


def setup_inputs():
    n = np.random.standard_normal
    s = mx_kscale(K)[:, None]
    packed_xT = pack_weight(n((K, T)) * s)
    return {
        "x_words": packed_xT[0],
        "x_scales": packed_xT[1],
        "w1": (n((K, N)) / np.sqrt(K) / s).astype(np.float32),
        "w2": (n((K, N)) / np.sqrt(K) / s).astype(np.float32),
        "tau": np.random.uniform(0.1, 0.9, (N, S)).astype(np.float32),
        "offs": striped8(np.stack([np.random.permutation(T)[:S] for _ in range(8)])),
        "obs": striped(np.random.permutation(T)[:S]),
        "at": striped8(np.stack([np.random.permutation(S) for _ in range(8)])),
    }


def reference(x_words, x_scales, w1, w2, tau, offs, obs, at):
    x_obs = unpack_weight(x_words, x_scales)[:, unstriped(obs)]
    e = mxq(f64(w2), 0, "e4m3").T @ x_obs
    xq = unpack_weight(x_words, x_scales)[np.arange(K)[:, None], runs(offs, K)]
    y = mxq(f64(w1), 0, "e4m3").T @ xq
    d = e[np.arange(N)[:, None], runs(at, N)] - y
    out_0 = f64(tau) * d - (d - relu(d))
    return (out_0,) + planes(out_0)

@@ -1,0 +1,206 @@
+from contextlib import ExitStack
+
+import concourse.mybir as mybir
+
+K, T, S, N = 512, 2048, 512, 512
+FLOPS = 2 * 2 * K * N * S
+
+F32 = mybir.dt.float32
+BF16 = mybir.dt.bfloat16
+I32 = mybir.dt.int32
+U32 = mybir.dt.uint32
+U16 = mybir.dt.uint16
+U8 = mybir.dt.uint8
+FP8X4 = mybir.dt.float8_e4m3fn_x4
+ALU = mybir.AluOpType
+
+P = 128
+PACK = 4
+HALF = N // 2
+CHUNKS = [(0, 256), (256, 128), (384, 128)]
+
+
+def tile_picked_pinball_none_po_kernel(
+    tc, x_words, x_scales, w1, w2, tau, offs, obs, at, out_0, out_1, out_2
+):
+    nc = tc.nc
+    with ExitStack() as ctx:
+        keep = ctx.enter_context(tc.tile_pool(name="keep", bufs=1))
+        psum = ctx.enter_context(tc.psum_pool(name="psum", bufs=1))
+
+        obs_l = keep.tile([P, S // 16], U16, name="obs_l")
+        offs_l = keep.tile([P, S // 16], U16, name="offs_l")
+        at_l = keep.tile([P, S // 16], U16, name="at_l")
+        xs = keep.tile([P, T], U8, name="xs", align_bytes=64)
+        xw = keep.tile([P, T], I32, name="xw", align_bytes=64)
+
+        nc.vector.memset(xs[:].bitcast(I32), 0)
+        nc.sync.dma_start(obs_l[:], obs)
+        nc.sync.dma_start(offs_l[:], offs)
+        xs_i = xs[:].bitcast(I32)
+        rows = x_scales[0].bitcast(I32)
+        xw_v = x_words[0].rearrange("p c r -> p (c r)").bitcast(I32)
+        nc.sync.dma_start(xw[:, 0:512], xw_v[:, 0:512])
+        nc.sync.dma_start(xs_i[0:128:16, :], rows[0:16:2, :])
+        nc.sync.dma_start(xs_i[1:128:16, :], rows[1:16:2, :])
+        nc.sync.dma_start(xs_i[2:128:32, :], rows[2:16:4, :])
+        nc.sync.dma_start(xs_i[3:128:32, :], rows[3:16:4, :])
+        nc.sync.dma_start(xw[:, 512:T], xw_v[:, 512:T])
+
+        def load_w(w, name):
+            halves = []
+            for h in range(2):
+                raw = keep.tile([P, PACK, HALF], F32, name="%s_raw%d" % (name, h), tag="%s_raw%d" % (name, h), align_bytes=64)
+                nc.sync.dma_start(
+                    raw[:], w.rearrange("(p j) c -> p j c", j=PACK)[:, :, h * HALF : (h + 1) * HALF]
+                )
+                halves.append(raw)
+            return halves
+
+        w2_raw = load_w(w2, "w2")
+        nc.sync.dma_start(at_l[:], at)
+        w1_raw = load_w(w1, "w1")
+
+        obs_s = keep.tile([P, S], U8, name="obs_s", align_bytes=64)
+        offs_g = keep.tile([P, S], U8, name="offs_g", align_bytes=64)
+        offs_s = keep.tile([P, S], U8, name="offs_s", align_bytes=64)
+        obs_w = keep.tile([P, S], U32, name="obs_w", align_bytes=64)
+        nc.vector.tensor_copy(offs_g[:], xs[:].indirect(offs_l[:]))
+        nc.vector.tensor_copy(obs_s[:], xs[:].indirect(obs_l[:]))
+        nc.vector.tensor_copy(offs_s[:].bitcast(I32), offs_g[:].bitcast(I32))
+        nc.vector.tensor_copy(obs_w[:], xw[:].bitcast(U32).indirect(obs_l[:]))
+        for r in range(2):
+            nc.sync.dma_start(
+                offs_s[:].bitcast(I32)[2 + r : 128 : 32, :], offs_g[:].bitcast(I32)[16 + r : 128 : 32, :]
+            )
+
+        tau_v = tau.rearrange("(p t) j -> p t j", t=PACK)
+        tau_h = []
+        for h in range(2):
+            tt = keep.tile([P, PACK, HALF], F32, name="tau%d" % h)
+            nc.sync.dma_start(tt[:], tau_v[:, :, h * HALF : (h + 1) * HALF])
+            tau_h.append(tt)
+
+        def cast_half(copy, wb, raw, h):
+            copy(
+                wb[:, :, h * 64 : (h + 1) * 64, :].rearrange("p t m j -> p m j t"),
+                raw[:].rearrange("p j (m t) -> p m j t", t=PACK),
+            )
+
+        def quant_w(wb, codes, scales, t0, t1):
+            cols = slice(t0 * P, t1 * P)
+            nc.vector.quantize_mx(
+                out=codes[:, cols].bitcast(FP8X4),
+                scales=scales[:, cols],
+                in_=wb[:, t0:t1, :, :].rearrange("p t m j -> p (t m j)"),
+            )
+
+        def product(dst, codes, scales, t, words, planes):
+            cols = slice(t * P, (t + 1) * P)
+            nc.tensor.matmul_mx(
+                out=dst,
+                lhsT=codes[:, cols].bitcast(FP8X4),
+                lhsT_scale=scales[:, cols],
+                rhs=words.bitcast(FP8X4),
+                rhs_scale=planes,
+                start=True,
+                stop=True,
+            )
+
+        w2b = keep.tile([P, PACK, P, PACK], BF16, name="w2b", align_bytes=64)
+        w2c = keep.tile([P, N], U32, name="w2c", align_bytes=64)
+        w2s = keep.tile([P, N], U8, name="w2s", align_bytes=64)
+        w1b = keep.tile([P, PACK, P, PACK], BF16, name="w1b", tag="reuse", align_bytes=64)
+        w1c = keep.tile([P, N], U32, name="w1c", align_bytes=64)
+        w1s = keep.tile([P, N], U8, name="w1s", align_bytes=64)
+        cast_half(nc.scalar.copy, w2b, w2_raw[0], 0)
+        cast_half(nc.vector.tensor_copy, w2b, w2_raw[1], 1)
+        for t0, t1 in ((0, 1), (1, 2), (2, 4)):
+            quant_w(w2b, w2c, w2s, t0, t1)
+        offs_w = keep.tile([P, S], U32, name="offs_w", tag="w2_raw1", align_bytes=64)
+        nc.vector.tensor_copy(offs_w[:], xw[:].bitcast(U32).indirect(offs_l[:]))
+        cast_half(nc.vector.tensor_copy, w1b, w1_raw[0], 0)
+        e_sb = []
+        for t in range(PACK):
+            e_ps = psum.tile([P, S], F32, name="e_ps%d" % t)
+            product(e_ps[:], w2c, w2s, t, obs_w[:], obs_s[:])
+            et = keep.tile([P, S], F32, name="e_sb%d" % t)
+            nc.scalar.copy(et[:], e_ps[:])
+            e_sb.append(et)
+            if t == 1:
+                cast_half(nc.scalar.copy, w1b, w1_raw[1], 1)
+
+        def look_up(dst, pair):
+            for i in range(2):
+                for h in range(2):
+                    nc.vector.tensor_copy(
+                        dst[:, i, h * HALF : (h + 1) * HALF],
+                        e_sb[2 * pair + i][:].indirect(at_l[:, h * 16 : (h + 1) * 16]),
+                    )
+
+        eg0 = keep.tile([P, 2, S], F32, name="eg0")
+        look_up(eg0, 0)
+        quant_w(w1b, w1c, w1s, 0, 4)
+        eg1 = keep.tile([P, 2, S], F32, name="eg1", tag="reuse", align_bytes=64)
+        look_up(eg1, 1)
+        eg = [eg0, eg1]
+
+        dn = []
+        for h in range(2):
+            cols = slice(h * HALF, (h + 1) * HALF)
+            dh = keep.tile([P, PACK, HALF], F32, name="dn%d" % h)
+            for pair in range(2):
+                y_ps = psum.tile([P, 2, HALF], F32, name="y_ps%d_%d" % (h, pair))
+                for i in range(2):
+                    product(y_ps[:, i, :], w1c, w1s, 2 * pair + i, offs_w[:, cols], offs_s[:, cols])
+                nc.vector.tensor_tensor(dh[:, 2 * pair : 2 * pair + 2, :], y_ps[:], eg[pair][:, :, cols], ALU.subtract)
+            dn.append(dh)
+
+        oc = keep.tile([P, S], U32, name="oc", align_bytes=64)
+        osc = keep.tile([P, S], U8, name="osc", align_bytes=64)
+        out_v = out_0.rearrange("(p t) j -> p t j", t=PACK)
+        words_v = out_1[0].rearrange("p c r -> p (c r)").bitcast(I32)
+        td = {}
+        rb = {}
+
+        def weigh(c):
+            c0, cw = CHUNKS[c]
+            h, lo = divmod(c0, HALF)
+            td[c] = keep.tile([P, PACK, cw], F32, name="td%d" % c)
+            nc.vector.tensor_tensor(td[c][:], dn[h][:, :, lo : lo + cw], tau_h[h][:, :, lo : lo + cw], ALU.mult)
+
+        def finish(c):
+            c0, cw = CHUNKS[c]
+            h, lo = divmod(c0, HALF)
+            res = keep.tile([P, PACK, cw], F32, name="res%d" % c)
+            nc.vector.scalar_tensor_tensor(
+                res[:], dn[h][:, :, lo : lo + cw], 0.0, td[c][:], ALU.max, ALU.subtract
+            )
+            nc.sync.dma_start(out_v[:, :, c0 : c0 + cw], res[:])
+            rb[c] = keep.tile([P, cw, PACK], BF16, name="rb%d" % c, align_bytes=64)
+            nc.scalar.copy(
+                rb[c][:].rearrange("p (a i) t -> p a t i", i=4),
+                res[:].rearrange("p t (a i) -> p a t i", i=4),
+            )
+
+        def hand_on(c):
+            c0, cw = CHUNKS[c]
+            nc.vector.quantize_mx(
+                out=oc[:, c0 : c0 + cw].bitcast(FP8X4),
+                scales=osc[:, c0 : c0 + cw],
+                in_=rb[c][:].rearrange("p a t -> p (a t)"),
+            )
+            nc.sync.dma_start(words_v[:, c0 : c0 + cw], oc[:, c0 : c0 + cw].bitcast(I32))
+
+        weigh(0)
+        weigh(1)
+        finish(0)
+        weigh(2)
+        finish(1)
+        finish(2)
+        for c in range(len(CHUNKS)):
+            hand_on(c)
+        srows = out_2[0].bitcast(I32)
+        for q in range(4):
+            queue = nc.scalar if q % 2 else nc.sync
+            queue.dma_start(srows[4 * q : 4 * q + 4, :], osc[:].bitcast(I32)[32 * q : 32 * q + 4, :])

@@ -1,6 +1,7 @@
 from contextlib import ExitStack
 
 import concourse.mybir as mybir
+from concourse.masks import make_identity
 
 K, T, S, N = 512, 2048, 512, 512
 FLOPS = 2 * 2 * K * N * S
@@ -13,11 +14,11 @@ U16 = mybir.dt.uint16
 U8 = mybir.dt.uint8
 FP8X4 = mybir.dt.float8_e4m3fn_x4
 ALU = mybir.AluOpType
+ACT = mybir.ActivationFunctionType
 
 P = 128
 PACK = 4
 HALF = N // 2
-CHUNKS = [(0, 256), (256, 128), (384, 128)]
 
 
 def tile_picked_pinball_none_po_kernel(
@@ -34,57 +35,52 @@ def tile_picked_pinball_none_po_kernel(
         xs = keep.tile([P, T], U8, name="xs", align_bytes=64)
         xw = keep.tile([P, T], I32, name="xw", align_bytes=64)
 
-        nc.vector.memset(xs[:].bitcast(I32), 0)
-        nc.sync.dma_start(obs_l[:], obs)
-        nc.sync.dma_start(offs_l[:], offs)
+        def load(raw, w, h):
+            nc.sync.dma_start(
+                raw[:].rearrange("p (j c) -> p j c", j=PACK),
+                w.rearrange("(p j) c -> p j c", j=PACK)[:, :, h * HALF : (h + 1) * HALF],
+            )
+
+        w2_raw = [keep.tile([P, PACK * HALF], F32, name="w2_raw%d" % h, align_bytes=64) for h in range(2)]
+        w1_raw = [keep.tile([P, PACK * HALF], F32, name="w1_raw%d" % h, align_bytes=64) for h in range(2)]
+
         xs_i = xs[:].bitcast(I32)
         rows = x_scales[0].bitcast(I32)
-        xw_v = x_words[0].rearrange("p c r -> p (c r)").bitcast(I32)
-        nc.sync.dma_start(xw[:, 0:512], xw_v[:, 0:512])
+        nc.vector.memset(xs_i, 0)
+        load(w2_raw[0], w2, 0)
+        nc.sync.dma_start(obs_l[:], obs)
+        nc.sync.dma_start(offs_l[:], offs)
         nc.sync.dma_start(xs_i[0:128:16, :], rows[0:16:2, :])
         nc.sync.dma_start(xs_i[1:128:16, :], rows[1:16:2, :])
         nc.sync.dma_start(xs_i[2:128:32, :], rows[2:16:4, :])
         nc.sync.dma_start(xs_i[3:128:32, :], rows[3:16:4, :])
-        nc.sync.dma_start(xw[:, 512:T], xw_v[:, 512:T])
-
-        def load_w(w, name):
-            halves = []
-            for h in range(2):
-                raw = keep.tile([P, PACK, HALF], F32, name="%s_raw%d" % (name, h), tag="%s_raw%d" % (name, h), align_bytes=64)
-                nc.sync.dma_start(
-                    raw[:], w.rearrange("(p j) c -> p j c", j=PACK)[:, :, h * HALF : (h + 1) * HALF]
-                )
-                halves.append(raw)
-            return halves
-
-        w2_raw = load_w(w2, "w2")
+        nc.sync.dma_start(xw[:], x_words[0].rearrange("p c r -> p (c r)").bitcast(I32))
+        load(w2_raw[1], w2, 1)
+        load(w1_raw[0], w1, 0)
+        load(w1_raw[1], w1, 1)
         nc.sync.dma_start(at_l[:], at)
-        w1_raw = load_w(w1, "w1")
 
         obs_s = keep.tile([P, S], U8, name="obs_s", align_bytes=64)
         offs_g = keep.tile([P, S], U8, name="offs_g", align_bytes=64)
         offs_s = keep.tile([P, S], U8, name="offs_s", align_bytes=64)
         obs_w = keep.tile([P, S], U32, name="obs_w", align_bytes=64)
+        nc.gpsimd.memset(offs_s[:].bitcast(I32), 0)
         nc.vector.tensor_copy(offs_g[:], xs[:].indirect(offs_l[:]))
         nc.vector.tensor_copy(obs_s[:], xs[:].indirect(obs_l[:]))
-        nc.vector.tensor_copy(offs_s[:].bitcast(I32), offs_g[:].bitcast(I32))
         nc.vector.tensor_copy(obs_w[:], xw[:].bitcast(U32).indirect(obs_l[:]))
-        for r in range(2):
-            nc.sync.dma_start(
-                offs_s[:].bitcast(I32)[2 + r : 128 : 32, :], offs_g[:].bitcast(I32)[16 + r : 128 : 32, :]
-            )
+        for r in range(4):
+            src = 16 * (r // 2) + r % 2
+            nc.scalar.dma_start(offs_s[:].bitcast(I32)[r:128:32, :], offs_g[:].bitcast(I32)[src:128:32, :])
 
         tau_v = tau.rearrange("(p t) j -> p t j", t=PACK)
-        tau_h = []
+        tau_sb = keep.tile([P, PACK, S], F32, name="tau_sb")
         for h in range(2):
-            tt = keep.tile([P, PACK, HALF], F32, name="tau%d" % h)
-            nc.sync.dma_start(tt[:], tau_v[:, :, h * HALF : (h + 1) * HALF])
-            tau_h.append(tt)
+            nc.sync.dma_start(tau_sb[:, 2 * h : 2 * h + 2, :], tau_v[:, 2 * h : 2 * h + 2, :])
 
-        def cast_half(copy, wb, raw, h):
+        def cast(copy, wb, raw, h, t0, t1):
             copy(
-                wb[:, :, h * 64 : (h + 1) * 64, :].rearrange("p t m j -> p m j t"),
-                raw[:].rearrange("p j (m t) -> p m j t", t=PACK),
+                wb[:, t0:t1, h * 64 : (h + 1) * 64, :].rearrange("p t m j -> p m j t"),
+                raw[:].rearrange("p (j m t) -> p m j t", j=PACK, t=PACK)[:, :, :, t0:t1],
             )
 
         def quant_w(wb, codes, scales, t0, t1):
@@ -110,97 +106,125 @@ def tile_picked_pinball_none_po_kernel(
         w2b = keep.tile([P, PACK, P, PACK], BF16, name="w2b", align_bytes=64)
         w2c = keep.tile([P, N], U32, name="w2c", align_bytes=64)
         w2s = keep.tile([P, N], U8, name="w2s", align_bytes=64)
-        w1b = keep.tile([P, PACK, P, PACK], BF16, name="w1b", tag="reuse", align_bytes=64)
+        w1b = keep.tile([P, PACK, P, PACK], BF16, name="w1b", align_bytes=64)
         w1c = keep.tile([P, N], U32, name="w1c", align_bytes=64)
         w1s = keep.tile([P, N], U8, name="w1s", align_bytes=64)
-        cast_half(nc.scalar.copy, w2b, w2_raw[0], 0)
-        cast_half(nc.vector.tensor_copy, w2b, w2_raw[1], 1)
+        cast(nc.scalar.copy, w2b, w2_raw[0], 0, 0, PACK)
+        cast(nc.scalar.copy, w2b, w2_raw[1], 1, 0, PACK)
+        offs_w = keep.tile([P, S], U32, name="offs_w", align_bytes=64)
+        nc.vector.tensor_copy(offs_w[:], xw[:].bitcast(U32).indirect(offs_l[:]))
         for t0, t1 in ((0, 1), (1, 2), (2, 4)):
             quant_w(w2b, w2c, w2s, t0, t1)
-        offs_w = keep.tile([P, S], U32, name="offs_w", tag="w2_raw1", align_bytes=64)
-        nc.vector.tensor_copy(offs_w[:], xw[:].bitcast(U32).indirect(offs_l[:]))
-        cast_half(nc.vector.tensor_copy, w1b, w1_raw[0], 0)
-        e_sb = []
-        for t in range(PACK):
-            e_ps = psum.tile([P, S], F32, name="e_ps%d" % t)
-            product(e_ps[:], w2c, w2s, t, obs_w[:], obs_s[:])
-            et = keep.tile([P, S], F32, name="e_sb%d" % t)
-            nc.scalar.copy(et[:], e_ps[:])
-            e_sb.append(et)
-            if t == 1:
-                cast_half(nc.scalar.copy, w1b, w1_raw[1], 1)
+        cast(nc.scalar.copy, w1b, w1_raw[0], 0, 0, PACK)
+        cast(nc.vector.tensor_copy, w1b, w1_raw[1], 1, 0, 2)
+        cast(nc.vector.tensor_copy, w1b, w1_raw[1], 1, 2, 4)
+        quant_w(w1b, w1c, w1s, 0, 2)
+        quant_w(w1b, w1c, w1s, 2, 4)
 
-        def look_up(dst, pair):
-            for i in range(2):
-                for h in range(2):
-                    nc.vector.tensor_copy(
-                        dst[:, i, h * HALF : (h + 1) * HALF],
-                        e_sb[2 * pair + i][:].indirect(at_l[:, h * 16 : (h + 1) * 16]),
+        window = [w1_raw[0], w1_raw[1], w2_raw[0], w2_raw[1]]
+        eg = keep.tile([P, S], F32, name="eg")
+        dn = keep.tile([P, PACK - 1, S], F32, name="dn")
+        td = keep.tile([P, PACK, S], F32, name="td")
+        res = keep.tile([P, PACK, S], F32, name="res")
+        y0 = keep.tile([P, S], F32, name="y0")
+        ident = keep.tile([P, P], F32, name="ident")
+        make_identity(nc, ident[:])
+
+        def target(t):
+            e_ps = psum.tile([P, S], F32, name="e_ps%d" % t, tag="bank%d" % t)
+            product(e_ps[:], w2c, w2s, t, obs_w[:], obs_s[:])
+            nc.scalar.mul(window[t][:, 0:S], e_ps[:], -1.0)
+
+        def forecast(t, dst):
+            y_ps = psum.tile([P, S], F32, name="y_ps%d" % t, tag="bank%d" % (t + 1 if t in (1, 2) else t + 4))
+            product(y_ps[:], w1c, w1s, t, offs_w[:], offs_s[:])
+            nc.scalar.copy(dst, y_ps[:])
+
+        def turn_sum(dst, terms):
+            for b in range(dst.shape[1] // P):
+                cols = slice(b * P, (b + 1) * P)
+                for i, term in enumerate(terms):
+                    nc.tensor.matmul(
+                        dst[:, cols], term[:, cols], ident[:], start=(i == 0), stop=(i == len(terms) - 1), is_transpose=True
                     )
 
-        eg0 = keep.tile([P, 2, S], F32, name="eg0")
-        look_up(eg0, 0)
-        quant_w(w1b, w1c, w1s, 0, 4)
-        eg1 = keep.tile([P, 2, S], F32, name="eg1", tag="reuse", align_bytes=64)
-        look_up(eg1, 1)
-        eg = [eg0, eg1]
-
-        dn = []
-        for h in range(2):
+        def weigh(h):
             cols = slice(h * HALF, (h + 1) * HALF)
-            dh = keep.tile([P, PACK, HALF], F32, name="dn%d" % h)
-            for pair in range(2):
-                y_ps = psum.tile([P, 2, HALF], F32, name="y_ps%d_%d" % (h, pair))
-                for i in range(2):
-                    product(y_ps[:, i, :], w1c, w1s, 2 * pair + i, offs_w[:, cols], offs_s[:, cols])
-                nc.vector.tensor_tensor(dh[:, 2 * pair : 2 * pair + 2, :], y_ps[:], eg[pair][:, :, cols], ALU.subtract)
-            dn.append(dh)
+            nc.vector.tensor_tensor(td[:, 1:PACK, cols], dn[:, :, cols], tau_sb[:, 1:PACK, cols], ALU.mult)
+
+        def compare(t):
+            nc.vector.tensor_tensor(dn[:, t - 1, :], window[t][:].indirect(at_l[:]), td[:, t - 1, :], ALU.add)
+
+        target(0)
+        target(1)
+        forecast(1, td[:, 0, :])
+        forecast(2, td[:, 1, :])
+        target(2)
+        target(3)
+        forecast(3, td[:, 2, :])
+        forecast(0, y0[:])
+        nc.vector.tensor_copy(eg[:], window[0][:].indirect(at_l[:]))
+        compare(1)
+        compare(2)
+        compare(3)
+
+        tau_ps = psum.tile([P, S], F32, name="tau_ps", tag="bank5")
+        turn_sum(tau_ps[:], [tau_sb[:, 0, :]])
+        nc.scalar.mul(td[:, 3, :], tau_ps[:], -1.0)
+        over = keep.tile([P, S], F32, name="over")
+        under = keep.tile([P, S], F32, name="under")
+
+        def first_plane(h):
+            cols = slice(h * HALF, (h + 1) * HALF)
+            d_ps = psum.tile([P, HALF], F32, name="d_ps%d" % h, tag="bank%d" % h)
+            turn_sum(d_ps[:], [eg[:, cols], y0[:, cols]])
+            nc.scalar.activation(over[:, cols], d_ps[:], ACT.Relu)
+            nc.vector.tensor_tensor(under[:, cols], d_ps[:], td[:, 3, cols], ALU.mult)
+            o_ps = psum.tile([P, HALF], F32, name="o_ps%d" % h, tag="bank%d" % (h + 2))
+            turn_sum(o_ps[:], [over[:, cols], under[:, cols]])
+            nc.scalar.copy(res[:, 0, cols], o_ps[:])
 
         oc = keep.tile([P, S], U32, name="oc", align_bytes=64)
         osc = keep.tile([P, S], U8, name="osc", align_bytes=64)
         out_v = out_0.rearrange("(p t) j -> p t j", t=PACK)
         words_v = out_1[0].rearrange("p c r -> p (c r)").bitcast(I32)
-        td = {}
-        rb = {}
+        rb = keep.tile([P, S, PACK], BF16, name="rb", align_bytes=64)
 
-        def weigh(c):
-            c0, cw = CHUNKS[c]
-            h, lo = divmod(c0, HALF)
-            td[c] = keep.tile([P, PACK, cw], F32, name="td%d" % c)
-            nc.vector.tensor_tensor(td[c][:], dn[h][:, :, lo : lo + cw], tau_h[h][:, :, lo : lo + cw], ALU.mult)
-
-        def finish(c):
-            c0, cw = CHUNKS[c]
-            h, lo = divmod(c0, HALF)
-            res = keep.tile([P, PACK, cw], F32, name="res%d" % c)
+        def finish(c0, c1, copy):
             nc.vector.scalar_tensor_tensor(
-                res[:], dn[h][:, :, lo : lo + cw], 0.0, td[c][:], ALU.max, ALU.subtract
+                res[:, 1:PACK, c0:c1], dn[:, :, c0:c1], 0.0, td[:, 1:PACK, c0:c1], ALU.max, ALU.subtract
             )
-            nc.sync.dma_start(out_v[:, :, c0 : c0 + cw], res[:])
-            rb[c] = keep.tile([P, cw, PACK], BF16, name="rb%d" % c, align_bytes=64)
-            nc.scalar.copy(
-                rb[c][:].rearrange("p (a i) t -> p a t i", i=4),
-                res[:].rearrange("p t (a i) -> p a t i", i=4),
+            copy(
+                rb[:, c0:c1, :].rearrange("p (a i) t -> p a t i", i=4),
+                res[:, :, c0:c1].rearrange("p t (a i) -> p a t i", i=4),
             )
 
-        def hand_on(c):
-            c0, cw = CHUNKS[c]
+        def store(c0, c1):
+            nc.sync.dma_start(out_v[:, :, c0:c1], res[:, :, c0:c1])
+
+        def hand_on(c0, c1):
             nc.vector.quantize_mx(
-                out=oc[:, c0 : c0 + cw].bitcast(FP8X4),
-                scales=osc[:, c0 : c0 + cw],
-                in_=rb[c][:].rearrange("p a t -> p (a t)"),
+                out=oc[:, c0:c1].bitcast(FP8X4),
+                scales=osc[:, c0:c1],
+                in_=rb[:, c0:c1, :].rearrange("p a t -> p (a t)"),
             )
-            nc.sync.dma_start(words_v[:, c0 : c0 + cw], oc[:, c0 : c0 + cw].bitcast(I32))
 
+        first_plane(0)
         weigh(0)
+        first_plane(1)
+        finish(0, 128, nc.scalar.copy)
+        finish(128, 256, nc.scalar.copy)
+        store(0, 256)
         weigh(1)
-        finish(0)
-        weigh(2)
-        finish(1)
-        finish(2)
-        for c in range(len(CHUNKS)):
-            hand_on(c)
+        finish(256, 384, nc.scalar.copy)
+        store(256, 384)
+        finish(384, 512, nc.vector.tensor_copy)
+        store(384, 512)
+        hand_on(0, 256)
+        nc.sync.dma_start(words_v[:, 0:HALF], oc[:, 0:HALF].bitcast(I32))
+        hand_on(256, 512)
+        nc.sync.dma_start(words_v[:, HALF:S], oc[:, HALF:S].bitcast(I32))
         srows = out_2[0].bitcast(I32)
         for q in range(4):
-            queue = nc.scalar if q % 2 else nc.sync
+            queue = nc.scalar if q else nc.sync
             queue.dma_start(srows[4 * q : 4 * q + 4, :], osc[:].bitcast(I32)[32 * q : 32 * q + 4, :])

@@ -171,6 +171,7 @@ def tile_picked_pinball_none_po_kernel(
         tau_ps = psum.tile([P, S], F32, name="tau_ps", tag="bank5")
         turn_sum(tau_ps[:], [tau_sb[:, 0, :]])
         nc.scalar.mul(td[:, 3, :], tau_ps[:], -1.0)
+        out_v = out_0.rearrange("(p t) j -> p t j", t=PACK)
         over = keep.tile([P, S], F32, name="over")
         under = keep.tile([P, S], F32, name="under")
 
@@ -183,10 +184,10 @@ def tile_picked_pinball_none_po_kernel(
             o_ps = psum.tile([P, HALF], F32, name="o_ps%d" % h, tag="bank%d" % (h + 2))
             turn_sum(o_ps[:], [over[:, cols], under[:, cols]])
             nc.scalar.copy(res[:, 0, cols], o_ps[:])
+            nc.sync.dma_start(out_v[:, 0, cols], res[:, 0, cols])
 
         oc = keep.tile([P, S], U32, name="oc", align_bytes=64)
         osc = keep.tile([P, S], U8, name="osc", align_bytes=64)
-        out_v = out_0.rearrange("(p t) j -> p t j", t=PACK)
         words_v = out_1[0].rearrange("p c r -> p (c r)").bitcast(I32)
         rb = keep.tile([P, S, PACK], BF16, name="rb", align_bytes=64)
 
@@ -194,13 +195,11 @@ def tile_picked_pinball_none_po_kernel(
             nc.vector.scalar_tensor_tensor(
                 res[:, 1:PACK, c0:c1], dn[:, :, c0:c1], 0.0, td[:, 1:PACK, c0:c1], ALU.max, ALU.subtract
             )
+            nc.sync.dma_start(out_v[:, 1:PACK, c0:c1], res[:, 1:PACK, c0:c1])
             copy(
                 rb[:, c0:c1, :].rearrange("p (a i) t -> p a t i", i=4),
                 res[:, :, c0:c1].rearrange("p t (a i) -> p a t i", i=4),
             )
-
-        def store(c0, c1):
-            nc.sync.dma_start(out_v[:, :, c0:c1], res[:, :, c0:c1])
 
         def hand_on(c0, c1):
             nc.vector.quantize_mx(
@@ -214,15 +213,13 @@ def tile_picked_pinball_none_po_kernel(
         first_plane(1)
         finish(0, 128, nc.scalar.copy)
         finish(128, 256, nc.scalar.copy)
-        store(0, 256)
         weigh(1)
         finish(256, 384, nc.scalar.copy)
-        store(256, 384)
         finish(384, 512, nc.vector.tensor_copy)
-        store(384, 512)
         hand_on(0, 256)
         nc.sync.dma_start(words_v[:, 0:HALF], oc[:, 0:HALF].bitcast(I32))
-        hand_on(256, 512)
+        hand_on(256, 384)
+        hand_on(384, 512)
         nc.sync.dma_start(words_v[:, HALF:S], oc[:, HALF:S].bitcast(I32))
         srows = out_2[0].bitcast(I32)
         for q in range(4):

@@ -18,7 +18,11 @@ ACT = mybir.ActivationFunctionType
 
 P = 128
 PACK = 4
-HALF = N // 2
+QUAD = 32
+GROUP = 16
+HALF = 256
+QUARTER = 128
+RUN = 4
 
 
 def tile_picked_pinball_none_po_kernel(
@@ -29,9 +33,9 @@ def tile_picked_pinball_none_po_kernel(
         keep = ctx.enter_context(tc.tile_pool(name="keep", bufs=1))
         psum = ctx.enter_context(tc.psum_pool(name="psum", bufs=1))
 
-        obs_l = keep.tile([P, S // 16], U16, name="obs_l")
-        offs_l = keep.tile([P, S // 16], U16, name="offs_l")
-        at_l = keep.tile([P, S // 16], U16, name="at_l")
+        obs_l = keep.tile([P, S // GROUP], U16, name="obs_l")
+        offs_l = keep.tile([P, S // GROUP], U16, name="offs_l")
+        at_l = keep.tile([P, S // GROUP], U16, name="at_l")
         xs = keep.tile([P, T], U8, name="xs", align_bytes=64)
         xw = keep.tile([P, T], I32, name="xw", align_bytes=64)
 
@@ -50,10 +54,10 @@ def tile_picked_pinball_none_po_kernel(
         load(w2_raw[0], w2, 0)
         nc.sync.dma_start(obs_l[:], obs)
         nc.sync.dma_start(offs_l[:], offs)
-        nc.sync.dma_start(xs_i[0:128:16, :], rows[0:16:2, :])
-        nc.sync.dma_start(xs_i[1:128:16, :], rows[1:16:2, :])
-        nc.sync.dma_start(xs_i[2:128:32, :], rows[2:16:4, :])
-        nc.sync.dma_start(xs_i[3:128:32, :], rows[3:16:4, :])
+        for r in range(2):
+            nc.sync.dma_start(xs_i[r:P:GROUP, :], rows[r:16:2, :])
+        for r in range(2, PACK):
+            nc.sync.dma_start(xs_i[r:P:QUAD, :], rows[r:16:PACK, :])
         nc.sync.dma_start(xw[:], x_words[0].rearrange("p c r -> p (c r)").bitcast(I32))
         load(w2_raw[1], w2, 1)
         load(w1_raw[0], w1, 0)
@@ -68,9 +72,9 @@ def tile_picked_pinball_none_po_kernel(
         nc.vector.tensor_copy(offs_g[:], xs[:].indirect(offs_l[:]))
         nc.vector.tensor_copy(obs_s[:], xs[:].indirect(obs_l[:]))
         nc.vector.tensor_copy(obs_w[:], xw[:].bitcast(U32).indirect(obs_l[:]))
-        for r in range(4):
-            src = 16 * (r // 2) + r % 2
-            nc.scalar.dma_start(offs_s[:].bitcast(I32)[r:128:32, :], offs_g[:].bitcast(I32)[src:128:32, :])
+        for r in range(PACK):
+            src = GROUP * (r // 2) + r % 2
+            nc.scalar.dma_start(offs_s[:].bitcast(I32)[r:P:QUAD, :], offs_g[:].bitcast(I32)[src:P:QUAD, :])
 
         tau_v = tau.rearrange("(p t) j -> p t j", t=PACK)
         tau_sb = keep.tile([P, PACK, S], F32, name="tau_sb")
@@ -78,8 +82,9 @@ def tile_picked_pinball_none_po_kernel(
             nc.sync.dma_start(tau_sb[:, 2 * h : 2 * h + 2, :], tau_v[:, 2 * h : 2 * h + 2, :])
 
         def cast(copy, wb, raw, h, t0, t1):
+            per_half = HALF // PACK
             copy(
-                wb[:, t0:t1, h * 64 : (h + 1) * 64, :].rearrange("p t m j -> p m j t"),
+                wb[:, t0:t1, h * per_half : (h + 1) * per_half, :].rearrange("p t m j -> p m j t"),
                 raw[:].rearrange("p (j m t) -> p m j t", j=PACK, t=PACK)[:, :, :, t0:t1],
             )
 
@@ -91,14 +96,14 @@ def tile_picked_pinball_none_po_kernel(
                 in_=wb[:, t0:t1, :, :].rearrange("p t m j -> p (t m j)"),
             )
 
-        def product(dst, codes, scales, t, words, planes):
+        def product(dst, codes, scales, t, x_codes, x_bytes):
             cols = slice(t * P, (t + 1) * P)
             nc.tensor.matmul_mx(
                 out=dst,
                 lhsT=codes[:, cols].bitcast(FP8X4),
                 lhsT_scale=scales[:, cols],
-                rhs=words.bitcast(FP8X4),
-                rhs_scale=planes,
+                rhs=x_codes.bitcast(FP8X4),
+                rhs_scale=x_bytes,
                 start=True,
                 stop=True,
             )
@@ -113,13 +118,13 @@ def tile_picked_pinball_none_po_kernel(
         cast(nc.scalar.copy, w2b, w2_raw[1], 1, 0, PACK)
         offs_w = keep.tile([P, S], U32, name="offs_w", align_bytes=64)
         nc.vector.tensor_copy(offs_w[:], xw[:].bitcast(U32).indirect(offs_l[:]))
-        for t0, t1 in ((0, 1), (1, 2), (2, 4)):
+        for t0, t1 in ((0, 1), (1, 2), (2, PACK)):
             quant_w(w2b, w2c, w2s, t0, t1)
         cast(nc.scalar.copy, w1b, w1_raw[0], 0, 0, PACK)
         cast(nc.vector.tensor_copy, w1b, w1_raw[1], 1, 0, 2)
-        cast(nc.vector.tensor_copy, w1b, w1_raw[1], 1, 2, 4)
+        cast(nc.vector.tensor_copy, w1b, w1_raw[1], 1, 2, PACK)
         quant_w(w1b, w1c, w1s, 0, 2)
-        quant_w(w1b, w1c, w1s, 2, 4)
+        quant_w(w1b, w1c, w1s, 2, PACK)
 
         window = [w1_raw[0], w1_raw[1], w2_raw[0], w2_raw[1]]
         eg = keep.tile([P, S], F32, name="eg")
@@ -130,13 +135,15 @@ def tile_picked_pinball_none_po_kernel(
         ident = keep.tile([P, P], F32, name="ident")
         make_identity(nc, ident[:])
 
+        y_bank = {1: 2, 2: 3, 3: 7, 0: 4}
+
         def target(t):
             e_ps = psum.tile([P, S], F32, name="e_ps%d" % t, tag="bank%d" % t)
             product(e_ps[:], w2c, w2s, t, obs_w[:], obs_s[:])
             nc.scalar.mul(window[t][:, 0:S], e_ps[:], -1.0)
 
         def forecast(t, dst):
-            y_ps = psum.tile([P, S], F32, name="y_ps%d" % t, tag="bank%d" % (t + 1 if t in (1, 2) else t + 4))
+            y_ps = psum.tile([P, S], F32, name="y_ps%d" % t, tag="bank%d" % y_bank[t])
             product(y_ps[:], w1c, w1s, t, offs_w[:], offs_s[:])
             nc.scalar.copy(dst, y_ps[:])
 
@@ -164,9 +171,8 @@ def tile_picked_pinball_none_po_kernel(
         forecast(3, td[:, 2, :])
         forecast(0, y0[:])
         nc.vector.tensor_copy(eg[:], window[0][:].indirect(at_l[:]))
-        compare(1)
-        compare(2)
-        compare(3)
+        for t in range(1, PACK):
+            compare(t)
 
         tau_ps = psum.tile([P, S], F32, name="tau_ps", tag="bank5")
         turn_sum(tau_ps[:], [tau_sb[:, 0, :]])
@@ -191,15 +197,25 @@ def tile_picked_pinball_none_po_kernel(
         words_v = out_1[0].rearrange("p c r -> p (c r)").bitcast(I32)
         rb = keep.tile([P, S, PACK], BF16, name="rb", align_bytes=64)
 
-        def finish(c0, c1, copy):
+        def loss(c0, c1):
             nc.vector.scalar_tensor_tensor(
                 res[:, 1:PACK, c0:c1], dn[:, :, c0:c1], 0.0, td[:, 1:PACK, c0:c1], ALU.max, ALU.subtract
             )
+
+        def store(c0, c1):
             nc.sync.dma_start(out_v[:, 1:PACK, c0:c1], res[:, 1:PACK, c0:c1])
+
+        def round_out(copy, c0, c1):
             copy(
-                rb[:, c0:c1, :].rearrange("p (a i) t -> p a t i", i=4),
-                res[:, :, c0:c1].rearrange("p t (a i) -> p a t i", i=4),
+                rb[:, c0:c1, :].rearrange("p (a i) t -> p a t i", i=RUN),
+                res[:, :, c0:c1].rearrange("p t (a i) -> p a t i", i=RUN),
             )
+
+        def finish(c):
+            c0, c1 = c * QUARTER, (c + 1) * QUARTER
+            loss(c0, c1)
+            store(c0, c1)
+            round_out(nc.scalar.copy, c0, c1)
 
         def hand_on(c0, c1):
             nc.vector.quantize_mx(
@@ -207,21 +223,26 @@ def tile_picked_pinball_none_po_kernel(
                 scales=osc[:, c0:c1],
                 in_=rb[:, c0:c1, :].rearrange("p a t -> p (a t)"),
             )
+            nc.sync.dma_start(words_v[:, c0:c1], oc[:, c0:c1].bitcast(I32))
 
         first_plane(0)
         weigh(0)
         first_plane(1)
-        finish(0, 128, nc.scalar.copy)
-        finish(128, 256, nc.scalar.copy)
+        finish(0)
         weigh(1)
-        finish(256, 384, nc.scalar.copy)
-        finish(384, 512, nc.vector.tensor_copy)
-        hand_on(0, 256)
-        nc.sync.dma_start(words_v[:, 0:HALF], oc[:, 0:HALF].bitcast(I32))
-        hand_on(256, 384)
-        hand_on(384, 512)
-        nc.sync.dma_start(words_v[:, HALF:S], oc[:, HALF:S].bitcast(I32))
+        finish(1)
+        finish(2)
+        last = S - QUARTER
+        eighths = [(last, last + QUARTER // 2), (last + QUARTER // 2, S)]
+        for c0, c1 in eighths:
+            loss(c0, c1)
+        store(last, S)
+        for c0, c1 in eighths:
+            round_out(nc.vector.tensor_copy, c0, c1)
+        hand_on(0, HALF)
+        hand_on(HALF, last)
+        hand_on(last, S)
         srows = out_2[0].bitcast(I32)
-        for q in range(4):
+        for q in range(P // QUAD):
             queue = nc.scalar if q else nc.sync
-            queue.dma_start(srows[4 * q : 4 * q + 4, :], osc[:].bitcast(I32)[32 * q : 32 * q + 4, :])
+            queue.dma_start(srows[PACK * q : PACK * (q + 1), :], osc[:].bitcast(I32)[QUAD * q : QUAD * q + PACK, :])

@@ -39,60 +39,47 @@ def tile_picked_pinball_none_po_kernel(
         xs = keep.tile([P, T], U8, name="xs", align_bytes=64)
         xw = keep.tile([P, T], I32, name="xw", align_bytes=64)
 
-        def load(raw, w, h):
-            nc.sync.dma_start(
-                raw[:].rearrange("p (j c) -> p j c", j=PACK),
-                w.rearrange("(p j) c -> p j c", j=PACK)[:, :, h * HALF : (h + 1) * HALF],
-            )
-
-        w2_raw = [keep.tile([P, PACK * HALF], F32, name="w2_raw%d" % h, align_bytes=64) for h in range(2)]
-        w1_raw = [keep.tile([P, PACK * HALF], F32, name="w1_raw%d" % h, align_bytes=64) for h in range(2)]
+        w2_raw = keep.tile([P, PACK * N], F32, name="w2_raw", align_bytes=64)
+        w2_v = w2.rearrange("(p j) c -> p (j c)", j=PACK)
+        over_w1 = ctx.enter_context(tc.tile_pool(name="over_w1", bufs=1))
+        w1_raw = over_w1.tile([P, PACK * N], F32, name="w1_raw", offset=0)
 
         xs_i = xs[:].bitcast(I32)
         rows = x_scales[0].bitcast(I32)
-        nc.vector.memset(xs_i, 0)
-        load(w2_raw[0], w2, 0)
+        nc.gpsimd.memset(xs_i, 0)
         nc.sync.dma_start(obs_l[:], obs)
         nc.sync.dma_start(offs_l[:], offs)
-        for r in range(2):
-            nc.sync.dma_start(xs_i[r:P:GROUP, :], rows[r:16:2, :])
-        for r in range(2, PACK):
-            nc.sync.dma_start(xs_i[r:P:QUAD, :], rows[r:16:PACK, :])
+        nc.sync.dma_start(w2_raw[:, 0:N], w2_v[:, 0:N])
+        nc.sync.dma_start(xs_i[0:P:8, :], rows)
         nc.sync.dma_start(xw[:], x_words[0].rearrange("p c r -> p (c r)").bitcast(I32))
-        load(w2_raw[1], w2, 1)
-        load(w1_raw[0], w1, 0)
-        load(w1_raw[1], w1, 1)
+        nc.sync.dma_start(w2_raw[:, N:], w2_v[:, N:])
+        nc.sync.dma_start(w1_raw[:], w1.rearrange("(p j) c -> p (j c)", j=PACK))
         nc.sync.dma_start(at_l[:], at)
 
-        obs_s = keep.tile([P, S], U8, name="obs_s", align_bytes=64)
-        offs_g = keep.tile([P, S], U8, name="offs_g", align_bytes=64)
-        offs_s = keep.tile([P, S], U8, name="offs_s", align_bytes=64)
+        picked = keep.tile([P, 2 * S], U8, name="picked", tag="picked_tau", align_bytes=64)
         obs_w = keep.tile([P, S], U32, name="obs_w", align_bytes=64)
-        nc.gpsimd.memset(offs_s[:].bitcast(I32), 0)
-        nc.vector.tensor_copy(offs_g[:], xs[:].indirect(offs_l[:]))
-        nc.vector.tensor_copy(obs_s[:], xs[:].indirect(obs_l[:]))
+        zero = keep.tile([P, 8], F32, name="zero")
+        nc.vector.memset(zero[:], 0.0)
+        spare = [keep.tile([P, 2 * S], F32, name="spare%d" % i, align_bytes=64) for i in range(1)]
+        for win in spare:
+            nc.scalar.mul(win[:, S:], zero[:, 0:1].to_broadcast([P, S]), 1.0)
+        nc.vector.tensor_copy(picked[:, 0:S], xs[:].indirect(obs_l[:]))
+        nc.vector.tensor_copy(picked[:, S:], xs[:].indirect(offs_l[:]))
+        offs_w = keep.tile([P, S], U32, name="offs_w", align_bytes=64)
         nc.vector.tensor_copy(obs_w[:], xw[:].bitcast(U32).indirect(obs_l[:]))
-        for r in range(PACK):
-            src = GROUP * (r // 2) + r % 2
-            nc.scalar.dma_start(offs_s[:].bitcast(I32)[r:P:QUAD, :], offs_g[:].bitcast(I32)[src:P:QUAD, :])
+        nc.vector.tensor_copy(offs_w[:], xw[:].bitcast(U32).indirect(offs_l[:]))
 
-        tau_v = tau.rearrange("(p t) j -> p t j", t=PACK)
-        tau_sb = keep.tile([P, PACK, S], F32, name="tau_sb")
-        for h in range(2):
-            nc.sync.dma_start(tau_sb[:, 2 * h : 2 * h + 2, :], tau_v[:, 2 * h : 2 * h + 2, :])
-
-        def cast(copy, wb, raw, h, t0, t1):
-            per_half = HALF // PACK
+        def cast(copy, wb, raw, m0, m1, t0, t1, first):
             copy(
-                wb[:, t0:t1, h * per_half : (h + 1) * per_half, :].rearrange("p t m j -> p m j t"),
-                raw[:].rearrange("p (j m t) -> p m j t", j=PACK, t=PACK)[:, :, :, t0:t1],
+                wb[:, t0:t1, m0:m1, :].rearrange("p t m j -> p m j t"),
+                raw[:].rearrange("p (j m t) -> p m j t", j=PACK, t=PACK)[:, m0 - first : m1 - first, :, t0:t1],
             )
 
         def quant_w(wb, codes, scales, t0, t1):
             cols = slice(t0 * P, t1 * P)
             nc.vector.quantize_mx(
                 out=codes[:, cols].bitcast(FP8X4),
-                scales=scales[:, cols],
+                scales=scales(t0, t1),
                 in_=wb[:, t0:t1, :, :].rearrange("p t m j -> p (t m j)"),
             )
 
@@ -101,7 +88,7 @@ def tile_picked_pinball_none_po_kernel(
             nc.tensor.matmul_mx(
                 out=dst,
                 lhsT=codes[:, cols].bitcast(FP8X4),
-                lhsT_scale=scales[:, cols],
+                lhsT_scale=scales(t, t + 1),
                 rhs=x_codes.bitcast(FP8X4),
                 rhs_scale=x_bytes,
                 start=True,
@@ -110,24 +97,42 @@ def tile_picked_pinball_none_po_kernel(
 
         w2b = keep.tile([P, PACK, P, PACK], BF16, name="w2b", align_bytes=64)
         w2c = keep.tile([P, N], U32, name="w2c", align_bytes=64)
-        w2s = keep.tile([P, N], U8, name="w2s", align_bytes=64)
-        w1b = keep.tile([P, PACK, P, PACK], BF16, name="w1b", align_bytes=64)
-        w1c = keep.tile([P, N], U32, name="w1c", align_bytes=64)
-        w1s = keep.tile([P, N], U8, name="w1s", align_bytes=64)
-        cast(nc.scalar.copy, w2b, w2_raw[0], 0, 0, PACK)
-        cast(nc.scalar.copy, w2b, w2_raw[1], 1, 0, PACK)
-        offs_w = keep.tile([P, S], U32, name="offs_w", align_bytes=64)
-        nc.vector.tensor_copy(offs_w[:], xw[:].bitcast(U32).indirect(offs_l[:]))
-        for t0, t1 in ((0, 1), (1, 2), (2, PACK)):
-            quant_w(w2b, w2c, w2s, t0, t1)
-        cast(nc.scalar.copy, w1b, w1_raw[0], 0, 0, PACK)
-        cast(nc.vector.tensor_copy, w1b, w1_raw[1], 1, 0, 2)
-        cast(nc.vector.tensor_copy, w1b, w1_raw[1], 1, 2, PACK)
-        quant_w(w1b, w1c, w1s, 0, 2)
-        quant_w(w1b, w1c, w1s, 2, PACK)
+        ws = keep.tile([P, N + HALF], U8, name="ws", align_bytes=64)
 
-        window = [w1_raw[0], w1_raw[1], w2_raw[0], w2_raw[1]]
-        eg = keep.tile([P, S], F32, name="eg")
+        def w2s(t0, t1):
+            return ws[:, t0 * P : t1 * P]
+
+        def w1s(t0, t1):
+            if t0 < 2:
+                return ws[PACK:P, (t0 + 1) * P : (t1 + 1) * P]
+            return ws[:, HALF + t0 * P : HALF + t1 * P]
+
+        w1b = keep.tile([P, PACK, P, PACK], BF16, name="w1b", tag="w1b_eg", align_bytes=64)
+        w1c = keep.tile([P, N], U32, name="w1c", align_bytes=64)
+        cast(nc.scalar.copy, w2b, w2_raw, 0, 72, 0, PACK, 0)
+        cast(nc.vector.tensor_copy, w2b, w2_raw, 72, P, 2, PACK, 0)
+        cast(nc.vector.tensor_copy, w2b, w2_raw, 72, P, 0, 2, 0)
+        quant_w(w2b, w2c, w2s, 2, PACK)
+        quant_w(w2b, w2c, w2s, 0, 2)
+        planes = keep.tile([P, 2 * S], U8, name="planes", align_bytes=64)
+        nc.gpsimd.memset(planes[:].bitcast(I32), 0)
+        for r in range(PACK):
+            nc.scalar.dma_start(planes[:].bitcast(I32)[r:P:QUAD, :], picked[:].bitcast(I32)[8 * r : P : QUAD, :])
+        obs_s = planes[:, 0:S]
+        offs_s = planes[:, S:]
+        tau_v = tau.rearrange("(p t) j -> p t j", t=PACK)
+        tau_sb = keep.tile([P, PACK, S], F32, name="tau_sb", tag="picked_tau", align_bytes=64)
+        for h in (1, 0):
+            nc.sync.dma_start(tau_sb[:, 2 * h : 2 * h + 2, :], tau_v[:, 2 * h : 2 * h + 2, :])
+        cast(nc.scalar.copy, w1b, w1_raw, 0, 40, 0, PACK, 0)
+        cast(nc.vector.tensor_copy, w1b, w1_raw, 40, P, 0, 2, 0)
+        cast(nc.vector.tensor_copy, w1b, w1_raw, 40, P, 2, PACK, 0)
+        for t0, t1 in ((0, 1), (1, 2), (2, PACK)):
+            quant_w(w1b, w1c, w1s, t0, t1)
+
+        late = [over_w1.tile([P, 2 * S], F32, name="late%d" % i, offset=i * 2 * S * 4) for i in range(2)]
+        window = [late[1], w2_raw, spare[0], late[0]]
+        eg = keep.tile([P, S], F32, name="eg", tag="w1b_eg", align_bytes=64)
         dn = keep.tile([P, PACK - 1, S], F32, name="dn")
         td = keep.tile([P, PACK, S], F32, name="td")
         res = keep.tile([P, PACK, S], F32, name="res")
@@ -135,16 +140,16 @@ def tile_picked_pinball_none_po_kernel(
         ident = keep.tile([P, P], F32, name="ident")
         make_identity(nc, ident[:])
 
-        y_bank = {1: 2, 2: 3, 3: 7, 0: 4}
+        y_bank = {0: 4, 1: 5, 2: 6, 3: 7}
 
         def target(t):
             e_ps = psum.tile([P, S], F32, name="e_ps%d" % t, tag="bank%d" % t)
-            product(e_ps[:], w2c, w2s, t, obs_w[:], obs_s[:])
+            product(e_ps[:], w2c, w2s, t, obs_w[:], obs_s)
             nc.scalar.mul(window[t][:, 0:S], e_ps[:], -1.0)
 
         def forecast(t, dst):
             y_ps = psum.tile([P, S], F32, name="y_ps%d" % t, tag="bank%d" % y_bank[t])
-            product(y_ps[:], w1c, w1s, t, offs_w[:], offs_s[:])
+            product(y_ps[:], w1c, w1s, t, offs_w[:], offs_s)
             nc.scalar.copy(dst, y_ps[:])
 
         def turn_sum(dst, terms):
@@ -157,26 +162,25 @@ def tile_picked_pinball_none_po_kernel(
 
         def weigh(h):
             cols = slice(h * HALF, (h + 1) * HALF)
-            nc.vector.tensor_tensor(td[:, 1:PACK, cols], dn[:, :, cols], tau_sb[:, 1:PACK, cols], ALU.mult)
+            nc.vector.tensor_tensor(td[:, 0:3, cols], dn[:, :, cols], tau_sb[:, 0:3, cols], ALU.mult)
 
         def compare(t):
-            nc.vector.tensor_tensor(dn[:, t - 1, :], window[t][:].indirect(at_l[:]), td[:, t - 1, :], ALU.add)
+            nc.vector.tensor_tensor(dn[:, t, :], window[t][:].indirect(at_l[:]), td[:, t + 1, :], ALU.add)
 
-        target(0)
-        target(1)
-        forecast(1, td[:, 0, :])
-        forecast(2, td[:, 1, :])
-        target(2)
         target(3)
-        forecast(3, td[:, 2, :])
-        forecast(0, y0[:])
-        nc.vector.tensor_copy(eg[:], window[0][:].indirect(at_l[:]))
-        for t in range(1, PACK):
+        target(0)
+        for t in range(3):
+            forecast(t, td[:, t + 1, :])
+            if t < 2:
+                target(t + 1)
+        forecast(3, y0[:])
+        nc.vector.tensor_copy(eg[:], window[3][:].indirect(at_l[:]))
+        for t in range(3):
             compare(t)
 
-        tau_ps = psum.tile([P, S], F32, name="tau_ps", tag="bank5")
-        turn_sum(tau_ps[:], [tau_sb[:, 0, :]])
-        nc.scalar.mul(td[:, 3, :], tau_ps[:], -1.0)
+        tau_ps = psum.tile([P, S], F32, name="tau_ps", tag="bank4")
+        turn_sum(tau_ps[:], [tau_sb[:, 3, :]])
+        nc.scalar.mul(td[:, 0, :], tau_ps[:], -1.0)
         out_v = out_0.rearrange("(p t) j -> p t j", t=PACK)
         over = keep.tile([P, S], F32, name="over")
         under = keep.tile([P, S], F32, name="under")
@@ -186,11 +190,11 @@ def tile_picked_pinball_none_po_kernel(
             d_ps = psum.tile([P, HALF], F32, name="d_ps%d" % h, tag="bank%d" % h)
             turn_sum(d_ps[:], [eg[:, cols], y0[:, cols]])
             nc.scalar.activation(over[:, cols], d_ps[:], ACT.Relu)
-            nc.vector.tensor_tensor(under[:, cols], d_ps[:], td[:, 3, cols], ALU.mult)
+            nc.vector.tensor_tensor(under[:, cols], d_ps[:], td[:, 0, cols], ALU.mult)
             o_ps = psum.tile([P, HALF], F32, name="o_ps%d" % h, tag="bank%d" % (h + 2))
             turn_sum(o_ps[:], [over[:, cols], under[:, cols]])
-            nc.scalar.copy(res[:, 0, cols], o_ps[:])
-            nc.sync.dma_start(out_v[:, 0, cols], res[:, 0, cols])
+            nc.scalar.copy(res[:, 3, cols], o_ps[:])
+            nc.sync.dma_start(out_v[:, 3, cols], res[:, 3, cols])
 
         oc = keep.tile([P, S], U32, name="oc", align_bytes=64)
         osc = keep.tile([P, S], U8, name="osc", align_bytes=64)
@@ -199,11 +203,11 @@ def tile_picked_pinball_none_po_kernel(
 
         def loss(c0, c1):
             nc.vector.scalar_tensor_tensor(
-                res[:, 1:PACK, c0:c1], dn[:, :, c0:c1], 0.0, td[:, 1:PACK, c0:c1], ALU.max, ALU.subtract
+                res[:, 0:3, c0:c1], dn[:, :, c0:c1], 0.0, td[:, 0:3, c0:c1], ALU.max, ALU.subtract
             )
 
         def store(c0, c1):
-            nc.sync.dma_start(out_v[:, 1:PACK, c0:c1], res[:, 1:PACK, c0:c1])
+            nc.sync.dma_start(out_v[:, 0:3, c0:c1], res[:, 0:3, c0:c1])
 
         def round_out(copy, c0, c1):
             copy(
@@ -214,7 +218,8 @@ def tile_picked_pinball_none_po_kernel(
         def finish(c):
             c0, c1 = c * QUARTER, (c + 1) * QUARTER
             loss(c0, c1)
-            store(c0, c1)
+            if c1 <= HALF:
+                store(c0, c1)
             round_out(nc.scalar.copy, c0, c1)
 
         def hand_on(c0, c1):
@@ -229,19 +234,18 @@ def tile_picked_pinball_none_po_kernel(
         weigh(0)
         first_plane(1)
         finish(0)
-        weigh(1)
         finish(1)
+        weigh(1)
         finish(2)
         last = S - QUARTER
         eighths = [(last, last + QUARTER // 2), (last + QUARTER // 2, S)]
         for c0, c1 in eighths:
             loss(c0, c1)
-        store(last, S)
+        store(HALF, S)
         for c0, c1 in eighths:
             round_out(nc.vector.tensor_copy, c0, c1)
         hand_on(0, HALF)
-        hand_on(HALF, last)
-        hand_on(last, S)
+        hand_on(HALF, S)
         srows = out_2[0].bitcast(I32)
         for q in range(P // QUAD):
             queue = nc.scalar if q else nc.sync

@@ -124,9 +124,9 @@ def tile_picked_pinball_none_po_kernel(
         tau_sb = keep.tile([P, PACK, S], F32, name="tau_sb", tag="picked_tau", align_bytes=64)
         for h in (1, 0):
             nc.sync.dma_start(tau_sb[:, 2 * h : 2 * h + 2, :], tau_v[:, 2 * h : 2 * h + 2, :])
-        cast(nc.scalar.copy, w1b, w1_raw, 0, 40, 0, PACK, 0)
-        cast(nc.vector.tensor_copy, w1b, w1_raw, 40, P, 0, 2, 0)
-        cast(nc.vector.tensor_copy, w1b, w1_raw, 40, P, 2, PACK, 0)
+        cast(nc.scalar.copy, w1b, w1_raw, 0, 32, 0, PACK, 0)
+        cast(nc.vector.tensor_copy, w1b, w1_raw, 32, P, 0, 2, 0)
+        cast(nc.vector.tensor_copy, w1b, w1_raw, 32, P, 2, PACK, 0)
         for t0, t1 in ((0, 1), (1, 2), (2, PACK)):
             quant_w(w1b, w1c, w1s, t0, t1)
 
@@ -150,7 +150,9 @@ def tile_picked_pinball_none_po_kernel(
         def forecast(t, dst):
             y_ps = psum.tile([P, S], F32, name="y_ps%d" % t, tag="bank%d" % y_bank[t])
             product(y_ps[:], w1c, w1s, t, offs_w[:], offs_s)
-            nc.scalar.copy(dst, y_ps[:])
+            step = HALF if t == 3 else S
+            for c0 in range(0, S, step):
+                nc.scalar.copy(dst[:, c0 : c0 + step], y_ps[:, c0 : c0 + step])
 
         def turn_sum(dst, terms):
             for b in range(dst.shape[1] // P):
@@ -248,5 +250,5 @@ def tile_picked_pinball_none_po_kernel(
         hand_on(HALF, S)
         srows = out_2[0].bitcast(I32)
         for q in range(P // QUAD):
-            queue = nc.scalar if q else nc.sync
+            queue = nc.scalar if q % 2 else nc.sync
             queue.dma_start(srows[PACK * q : PACK * (q + 1), :], osc[:].bitcast(I32)[QUAD * q : QUAD * q + PACK, :])

@@ -20,8 +20,13 @@ P = 128
 PACK = 4
 QUAD = 32
 GROUP = 16
+ROW_STEP = 8
+FUSED = 3
+TURNED = 3
 HALF = 256
 QUARTER = 128
+EIGHTH = 64
+W2_ON_SCALAR = 64
 RUN = 4
 
 
@@ -45,12 +50,11 @@ def tile_picked_pinball_none_po_kernel(
         w1_raw = over_w1.tile([P, PACK * N], F32, name="w1_raw", offset=0)
 
         xs_i = xs[:].bitcast(I32)
-        rows = x_scales[0].bitcast(I32)
         nc.gpsimd.memset(xs_i, 0)
         nc.sync.dma_start(obs_l[:], obs)
         nc.sync.dma_start(offs_l[:], offs)
         nc.sync.dma_start(w2_raw[:, 0:N], w2_v[:, 0:N])
-        nc.sync.dma_start(xs_i[0:P:8, :], rows)
+        nc.sync.dma_start(xs_i[0:P:ROW_STEP, :], x_scales[0].bitcast(I32))
         nc.sync.dma_start(xw[:], x_words[0].rearrange("p c r -> p (c r)").bitcast(I32))
         nc.sync.dma_start(w2_raw[:, N:], w2_v[:, N:])
         nc.sync.dma_start(w1_raw[:], w1.rearrange("(p j) c -> p (j c)", j=PACK))
@@ -60,19 +64,19 @@ def tile_picked_pinball_none_po_kernel(
         obs_w = keep.tile([P, S], U32, name="obs_w", align_bytes=64)
         zero = keep.tile([P, 8], F32, name="zero")
         nc.vector.memset(zero[:], 0.0)
-        spare = [keep.tile([P, 2 * S], F32, name="spare%d" % i, align_bytes=64) for i in range(1)]
-        for win in spare:
-            nc.scalar.mul(win[:, S:], zero[:, 0:1].to_broadcast([P, S]), 1.0)
+        first_window = keep.tile([P, 2 * S], F32, name="first_window", align_bytes=64)
+        nc.scalar.mul(first_window[:, S:], zero[:, 0:1].to_broadcast([P, S]), 1.0)
+
         nc.vector.tensor_copy(picked[:, 0:S], xs[:].indirect(obs_l[:]))
         nc.vector.tensor_copy(picked[:, S:], xs[:].indirect(offs_l[:]))
         offs_w = keep.tile([P, S], U32, name="offs_w", align_bytes=64)
         nc.vector.tensor_copy(obs_w[:], xw[:].bitcast(U32).indirect(obs_l[:]))
         nc.vector.tensor_copy(offs_w[:], xw[:].bitcast(U32).indirect(offs_l[:]))
 
-        def cast(copy, wb, raw, m0, m1, t0, t1, first):
+        def cast(copy, wb, raw, m0, m1, t0, t1):
             copy(
                 wb[:, t0:t1, m0:m1, :].rearrange("p t m j -> p m j t"),
-                raw[:].rearrange("p (j m t) -> p m j t", j=PACK, t=PACK)[:, m0 - first : m1 - first, :, t0:t1],
+                raw[:].rearrange("p (j m t) -> p m j t", j=PACK, t=PACK)[:, m0:m1, :, t0:t1],
             )
 
         def quant_w(wb, codes, scales, t0, t1):
@@ -97,7 +101,7 @@ def tile_picked_pinball_none_po_kernel(
 
         w2b = keep.tile([P, PACK, P, PACK], BF16, name="w2b", align_bytes=64)
         w2c = keep.tile([P, N], U32, name="w2c", align_bytes=64)
-        ws = keep.tile([P, N + HALF], U8, name="ws", align_bytes=64)
+        ws = keep.tile([P, N + 2 * P], U8, name="ws", align_bytes=64)
 
         def w2s(t0, t1):
             return ws[:, t0 * P : t1 * P]
@@ -105,52 +109,51 @@ def tile_picked_pinball_none_po_kernel(
         def w1s(t0, t1):
             if t0 < 2:
                 return ws[PACK:P, (t0 + 1) * P : (t1 + 1) * P]
-            return ws[:, HALF + t0 * P : HALF + t1 * P]
+            return ws[:, (t0 + 2) * P : (t1 + 2) * P]
 
         w1b = keep.tile([P, PACK, P, PACK], BF16, name="w1b", tag="w1b_eg", align_bytes=64)
         w1c = keep.tile([P, N], U32, name="w1c", align_bytes=64)
-        cast(nc.scalar.copy, w2b, w2_raw, 0, 72, 0, PACK, 0)
-        cast(nc.vector.tensor_copy, w2b, w2_raw, 72, P, 2, PACK, 0)
-        cast(nc.vector.tensor_copy, w2b, w2_raw, 72, P, 0, 2, 0)
+        cast(nc.scalar.copy, w2b, w2_raw, 0, W2_ON_SCALAR, 0, PACK)
+        cast(nc.vector.tensor_copy, w2b, w2_raw, W2_ON_SCALAR, P, 2, PACK)
+        cast(nc.vector.tensor_copy, w2b, w2_raw, W2_ON_SCALAR, P, 0, 2)
         quant_w(w2b, w2c, w2s, 2, PACK)
         quant_w(w2b, w2c, w2s, 0, 2)
-        planes = keep.tile([P, 2 * S], U8, name="planes", align_bytes=64)
-        nc.gpsimd.memset(planes[:].bitcast(I32), 0)
+
+        xq_s = keep.tile([P, 2 * S], U8, name="xq_s", align_bytes=64)
+        nc.gpsimd.memset(xq_s[:].bitcast(I32), 0)
         for r in range(PACK):
-            nc.scalar.dma_start(planes[:].bitcast(I32)[r:P:QUAD, :], picked[:].bitcast(I32)[8 * r : P : QUAD, :])
-        obs_s = planes[:, 0:S]
-        offs_s = planes[:, S:]
+            nc.scalar.dma_start(xq_s[:].bitcast(I32)[r:P:QUAD, :], picked[:].bitcast(I32)[ROW_STEP * r : P : QUAD, :])
+        obs_s = xq_s[:, 0:S]
+        offs_s = xq_s[:, S:]
+
         tau_v = tau.rearrange("(p t) j -> p t j", t=PACK)
         tau_sb = keep.tile([P, PACK, S], F32, name="tau_sb", tag="picked_tau", align_bytes=64)
-        for h in (1, 0):
-            nc.sync.dma_start(tau_sb[:, 2 * h : 2 * h + 2, :], tau_v[:, 2 * h : 2 * h + 2, :])
-        cast(nc.scalar.copy, w1b, w1_raw, 0, 32, 0, PACK, 0)
-        cast(nc.vector.tensor_copy, w1b, w1_raw, 32, P, 0, 2, 0)
-        cast(nc.vector.tensor_copy, w1b, w1_raw, 32, P, 2, PACK, 0)
+        for t0 in (2, 0):
+            nc.sync.dma_start(tau_sb[:, t0 : t0 + 2, :], tau_v[:, t0 : t0 + 2, :])
+
+        cast(nc.vector.tensor_copy, w1b, w1_raw, 0, P, 0, 2)
+        cast(nc.vector.tensor_copy, w1b, w1_raw, 0, P, 2, PACK)
         for t0, t1 in ((0, 1), (1, 2), (2, PACK)):
             quant_w(w1b, w1c, w1s, t0, t1)
 
-        late = [over_w1.tile([P, 2 * S], F32, name="late%d" % i, offset=i * 2 * S * 4) for i in range(2)]
-        window = [late[1], w2_raw, spare[0], late[0]]
+        on_w1 = [over_w1.tile([P, 2 * S], F32, name="on_w1_%d" % i, offset=i * 2 * S * 4) for i in range(2)]
+        window = [w2_raw, on_w1[0], on_w1[1], first_window]
         eg = keep.tile([P, S], F32, name="eg", tag="w1b_eg", align_bytes=64)
-        dn = keep.tile([P, PACK - 1, S], F32, name="dn")
+        dn = keep.tile([P, FUSED, S], F32, name="dn")
         td = keep.tile([P, PACK, S], F32, name="td")
         res = keep.tile([P, PACK, S], F32, name="res")
-        y0 = keep.tile([P, S], F32, name="y0")
+        y_turned = keep.tile([P, S], F32, name="y_turned")
         ident = keep.tile([P, P], F32, name="ident")
         make_identity(nc, ident[:])
-
-        y_bank = {0: 4, 1: 5, 2: 6, 3: 7}
 
         def target(t):
             e_ps = psum.tile([P, S], F32, name="e_ps%d" % t, tag="bank%d" % t)
             product(e_ps[:], w2c, w2s, t, obs_w[:], obs_s)
             nc.scalar.mul(window[t][:, 0:S], e_ps[:], -1.0)
 
-        def forecast(t, dst):
-            y_ps = psum.tile([P, S], F32, name="y_ps%d" % t, tag="bank%d" % y_bank[t])
+        def forecast(t, dst, step):
+            y_ps = psum.tile([P, S], F32, name="y_ps%d" % t, tag="bank%d" % (PACK + t))
             product(y_ps[:], w1c, w1s, t, offs_w[:], offs_s)
-            step = HALF if t == 3 else S
             for c0 in range(0, S, step):
                 nc.scalar.copy(dst[:, c0 : c0 + step], y_ps[:, c0 : c0 + step])
 
@@ -162,41 +165,37 @@ def tile_picked_pinball_none_po_kernel(
                         dst[:, cols], term[:, cols], ident[:], start=(i == 0), stop=(i == len(terms) - 1), is_transpose=True
                     )
 
-        def weigh(h):
-            cols = slice(h * HALF, (h + 1) * HALF)
-            nc.vector.tensor_tensor(td[:, 0:3, cols], dn[:, :, cols], tau_sb[:, 0:3, cols], ALU.mult)
+        def weigh(c0, c1):
+            nc.vector.tensor_tensor(td[:, 0:FUSED, c0:c1], dn[:, :, c0:c1], tau_sb[:, 0:FUSED, c0:c1], ALU.mult)
 
         def compare(t):
             nc.vector.tensor_tensor(dn[:, t, :], window[t][:].indirect(at_l[:]), td[:, t + 1, :], ALU.add)
 
-        target(3)
-        target(0)
-        for t in range(3):
-            forecast(t, td[:, t + 1, :])
-            if t < 2:
-                target(t + 1)
-        forecast(3, y0[:])
-        nc.vector.tensor_copy(eg[:], window[3][:].indirect(at_l[:]))
-        for t in range(3):
+        target(TURNED)
+        for t in range(FUSED):
+            target(t)
+            forecast(t, td[:, t + 1, :], S)
+        forecast(TURNED, y_turned[:], HALF)
+        nc.vector.tensor_copy(eg[:], window[TURNED][:].indirect(at_l[:]))
+        for t in range(FUSED):
             compare(t)
 
         tau_ps = psum.tile([P, S], F32, name="tau_ps", tag="bank4")
-        turn_sum(tau_ps[:], [tau_sb[:, 3, :]])
+        turn_sum(tau_ps[:], [tau_sb[:, TURNED, :]])
         nc.scalar.mul(td[:, 0, :], tau_ps[:], -1.0)
         out_v = out_0.rearrange("(p t) j -> p t j", t=PACK)
         over = keep.tile([P, S], F32, name="over")
         under = keep.tile([P, S], F32, name="under")
 
-        def first_plane(h):
+        def turned_plane(h):
             cols = slice(h * HALF, (h + 1) * HALF)
             d_ps = psum.tile([P, HALF], F32, name="d_ps%d" % h, tag="bank%d" % h)
-            turn_sum(d_ps[:], [eg[:, cols], y0[:, cols]])
+            turn_sum(d_ps[:], [eg[:, cols], y_turned[:, cols]])
             nc.scalar.activation(over[:, cols], d_ps[:], ACT.Relu)
             nc.vector.tensor_tensor(under[:, cols], d_ps[:], td[:, 0, cols], ALU.mult)
             o_ps = psum.tile([P, HALF], F32, name="o_ps%d" % h, tag="bank%d" % (h + 2))
             turn_sum(o_ps[:], [over[:, cols], under[:, cols]])
-            nc.scalar.copy(res[:, 3, cols], o_ps[:])
-            nc.sync.dma_start(out_v[:, 3, cols], res[:, 3, cols])
+            nc.scalar.copy(res[:, TURNED, cols], o_ps[:])
 
         oc = keep.tile([P, S], U32, name="oc", align_bytes=64)
         osc = keep.tile([P, S], U8, name="osc", align_bytes=64)
@@ -205,11 +204,11 @@ def tile_picked_pinball_none_po_kernel(
 
         def loss(c0, c1):
             nc.vector.scalar_tensor_tensor(
-                res[:, 0:3, c0:c1], dn[:, :, c0:c1], 0.0, td[:, 0:3, c0:c1], ALU.max, ALU.subtract
+                res[:, 0:FUSED, c0:c1], dn[:, :, c0:c1], 0.0, td[:, 0:FUSED, c0:c1], ALU.max, ALU.subtract
             )
 
         def store(c0, c1):
-            nc.sync.dma_start(out_v[:, 0:3, c0:c1], res[:, 0:3, c0:c1])
+            nc.sync.dma_start(out_v[:, 0:FUSED, c0:c1], res[:, 0:FUSED, c0:c1])
 
         def round_out(copy, c0, c1):
             copy(
@@ -220,34 +219,41 @@ def tile_picked_pinball_none_po_kernel(
         def finish(c):
             c0, c1 = c * QUARTER, (c + 1) * QUARTER
             loss(c0, c1)
-            if c1 <= HALF:
-                store(c0, c1)
+            store(c0, c1)
             round_out(nc.scalar.copy, c0, c1)
 
-        def hand_on(c0, c1):
+        def quant_out(c0, c1):
             nc.vector.quantize_mx(
                 out=oc[:, c0:c1].bitcast(FP8X4),
                 scales=osc[:, c0:c1],
                 in_=rb[:, c0:c1, :].rearrange("p a t -> p (a t)"),
             )
+
+        def store_words(c0, c1):
             nc.sync.dma_start(words_v[:, c0:c1], oc[:, c0:c1].bitcast(I32))
 
-        first_plane(0)
-        weigh(0)
-        first_plane(1)
-        finish(0)
-        finish(1)
-        weigh(1)
-        finish(2)
         last = S - QUARTER
-        eighths = [(last, last + QUARTER // 2), (last + QUARTER // 2, S)]
+        eighths = [(last, last + EIGHTH), (last + EIGHTH, S)]
+        turned_plane(0)
+        weigh(0, HALF)
+        turned_plane(1)
+        nc.sync.dma_start(out_v[:, TURNED, :], res[:, TURNED, :])
+        finish(0)
+        weigh(HALF, last)
+        finish(1)
+        finish(2)
+        for c0, c1 in eighths:
+            weigh(c0, c1)
         for c0, c1 in eighths:
             loss(c0, c1)
-        store(HALF, S)
-        for c0, c1 in eighths:
-            round_out(nc.vector.tensor_copy, c0, c1)
-        hand_on(0, HALF)
-        hand_on(HALF, S)
+        store(last, S)
+        round_out(nc.scalar.copy, *eighths[0])
+        quant_out(0, HALF)
+        store_words(0, HALF)
+        round_out(nc.vector.tensor_copy, *eighths[1])
+        quant_out(HALF, last)
+        quant_out(last, S)
+        store_words(HALF, S)
         srows = out_2[0].bitcast(I32)
         for q in range(P // QUAD):
             queue = nc.scalar if q % 2 else nc.sync

@@ -50,10 +50,10 @@ def tile_picked_pinball_none_po_kernel(
         w1_raw = over_w1.tile([P, PACK * N], F32, name="w1_raw", offset=0)
 
         xs_i = xs[:].bitcast(I32)
-        nc.gpsimd.memset(xs_i, 0)
+        nc.vector.memset(xs_i, 0)
+        nc.sync.dma_start(w2_raw[:, 0:N], w2_v[:, 0:N])
         nc.sync.dma_start(obs_l[:], obs)
         nc.sync.dma_start(offs_l[:], offs)
-        nc.sync.dma_start(w2_raw[:, 0:N], w2_v[:, 0:N])
         nc.sync.dma_start(xs_i[0:P:ROW_STEP, :], x_scales[0].bitcast(I32))
         nc.sync.dma_start(xw[:], x_words[0].rearrange("p c r -> p (c r)").bitcast(I32))
         nc.sync.dma_start(w2_raw[:, N:], w2_v[:, N:])
@@ -120,7 +120,7 @@ def tile_picked_pinball_none_po_kernel(
         quant_w(w2b, w2c, w2s, 0, 2)
 
         xq_s = keep.tile([P, 2 * S], U8, name="xq_s", align_bytes=64)
-        nc.gpsimd.memset(xq_s[:].bitcast(I32), 0)
+        nc.vector.memset(xq_s[:].bitcast(I32), 0)
         for r in range(PACK):
             nc.scalar.dma_start(xq_s[:].bitcast(I32)[r:P:QUAD, :], picked[:].bitcast(I32)[ROW_STEP * r : P : QUAD, :])
         obs_s = xq_s[:, 0:S]

@@ -151,19 +151,19 @@ def tile_picked_pinball_none_po_kernel(
             product(e_ps[:], w2c, w2s, t, obs_w[:], obs_s)
             nc.scalar.mul(window[t][:, 0:S], e_ps[:], -1.0)
 
-        def forecast(t, dst, step):
+        def forecast(t):
             y_ps = psum.tile([P, S], F32, name="y_ps%d" % t, tag="bank%d" % (PACK + t))
             product(y_ps[:], w1c, w1s, t, offs_w[:], offs_s)
-            for c0 in range(0, S, step):
-                nc.scalar.copy(dst[:, c0 : c0 + step], y_ps[:, c0 : c0 + step])
+            return y_ps
 
         def turn_sum(dst, terms):
-            for b in range(dst.shape[1] // P):
-                cols = slice(b * P, (b + 1) * P)
-                for i, term in enumerate(terms):
-                    nc.tensor.matmul(
-                        dst[:, cols], term[:, cols], ident[:], start=(i == 0), stop=(i == len(terms) - 1), is_transpose=True
-                    )
+            blocks = dst.shape[1] // P
+            for i, term in enumerate(terms):
+                for b in range(blocks):
+                    cols = slice(b * P, (b + 1) * P)
+                    first = i == 0 and b == 0
+                    final = i == len(terms) - 1 and b == blocks - 1
+                    nc.tensor.matmul(dst[:, cols], term[:, cols], ident[:], start=first, stop=final, is_transpose=True)
 
         def weigh(c0, c1):
             nc.vector.tensor_tensor(td[:, 0:FUSED, c0:c1], dn[:, :, c0:c1], tau_sb[:, 0:FUSED, c0:c1], ALU.mult)
@@ -172,10 +172,14 @@ def tile_picked_pinball_none_po_kernel(
             nc.vector.tensor_tensor(dn[:, t, :], window[t][:].indirect(at_l[:]), td[:, t + 1, :], ALU.add)
 
         target(TURNED)
-        for t in range(FUSED):
+        for t in range(FUSED - 1):
             target(t)
-            forecast(t, td[:, t + 1, :], S)
-        forecast(TURNED, y_turned[:], HALF)
+            nc.scalar.copy(td[:, t + 1, :], forecast(t)[:])
+        target(FUSED - 1)
+        y_last = forecast(TURNED)
+        nc.scalar.copy(y_turned[:, 0:HALF], y_last[:, 0:HALF])
+        nc.scalar.copy(td[:, FUSED, :], forecast(FUSED - 1)[:])
+        nc.scalar.copy(y_turned[:, HALF:], y_last[:, HALF:])
         nc.vector.tensor_copy(eg[:], window[TURNED][:].indirect(at_l[:]))
         for t in range(FUSED):
             compare(t)

@@ -1,7 +1,6 @@
 from contextlib import ExitStack
 
 import concourse.mybir as mybir
-from concourse.masks import make_identity
 
 K, T, S, N = 512, 2048, 512, 512
 FLOPS = 2 * 2 * K * N * S
@@ -21,12 +20,9 @@ PACK = 4
 QUAD = 32
 GROUP = 16
 ROW_STEP = 8
-FUSED = 3
-TURNED = 3
 HALF = 256
 QUARTER = 128
 EIGHTH = 64
-W2_ON_SCALAR = 64
 RUN = 4
 
 
@@ -41,50 +37,59 @@ def tile_picked_pinball_none_po_kernel(
         obs_l = keep.tile([P, S // GROUP], U16, name="obs_l")
         offs_l = keep.tile([P, S // GROUP], U16, name="offs_l")
         at_l = keep.tile([P, S // GROUP], U16, name="at_l")
-        xs = keep.tile([P, T], U8, name="xs", align_bytes=64)
+        xs_obs = keep.tile([P, T], U8, name="xs_obs", tag="xs_w1", align_bytes=64)
+        xs_offs = keep.tile([P, T], U8, name="xs_offs", tag="xs_tau", align_bytes=64)
         xw = keep.tile([P, T], I32, name="xw", align_bytes=64)
-
-        w2_raw = keep.tile([P, PACK * N], F32, name="w2_raw", align_bytes=64)
+        w2_raw = keep.tile([P, PACK * N], F32, name="w2_raw", tag="window1", align_bytes=64)
         w2_v = w2.rearrange("(p j) c -> p (j c)", j=PACK)
-        over_w1 = ctx.enter_context(tc.tile_pool(name="over_w1", bufs=1))
-        w1_raw = over_w1.tile([P, PACK * N], F32, name="w1_raw", offset=0)
-
-        xs_i = xs[:].bitcast(I32)
-        nc.vector.memset(xs_i, 0)
+        obs_s = keep.tile([P, S], U8, name="obs_s", align_bytes=64)
+        offs_s = keep.tile([P, S], U8, name="offs_s", align_bytes=64)
+        for plane in (xs_obs, obs_s, offs_s):
+            nc.vector.memset(plane[:].bitcast(I32), 0)
         nc.sync.dma_start(w2_raw[:, 0:N], w2_v[:, 0:N])
         nc.sync.dma_start(obs_l[:], obs)
         nc.sync.dma_start(offs_l[:], offs)
-        nc.sync.dma_start(xs_i[0:P:ROW_STEP, :], x_scales[0].bitcast(I32))
-        nc.sync.dma_start(xw[:], x_words[0].rearrange("p c r -> p (c r)").bitcast(I32))
+        nc.sync.dma_start(xs_obs[:].bitcast(I32)[0:P:ROW_STEP, :], x_scales[0].bitcast(I32))
         nc.sync.dma_start(w2_raw[:, N:], w2_v[:, N:])
-        nc.sync.dma_start(w1_raw[:], w1.rearrange("(p j) c -> p (j c)", j=PACK))
+        nc.sync.dma_start(xw[:], x_words[0].rearrange("p c r -> p (c r)").bitcast(I32))
         nc.sync.dma_start(at_l[:], at)
 
-        picked = keep.tile([P, 2 * S], U8, name="picked", tag="picked_tau", align_bytes=64)
-        obs_w = keep.tile([P, S], U32, name="obs_w", align_bytes=64)
         zero = keep.tile([P, 8], F32, name="zero")
         nc.vector.memset(zero[:], 0.0)
-        first_window = keep.tile([P, 2 * S], F32, name="first_window", align_bytes=64)
+        first_window = keep.tile([P, 2 * S], F32, name="first_window", tag="window0", align_bytes=64)
         nc.scalar.mul(first_window[:, S:], zero[:, 0:1].to_broadcast([P, S]), 1.0)
 
-        nc.vector.tensor_copy(picked[:, 0:S], xs[:].indirect(obs_l[:]))
-        nc.vector.tensor_copy(picked[:, S:], xs[:].indirect(offs_l[:]))
-        offs_w = keep.tile([P, S], U32, name="offs_w", align_bytes=64)
-        nc.vector.tensor_copy(obs_w[:], xw[:].bitcast(U32).indirect(obs_l[:]))
-        nc.vector.tensor_copy(offs_w[:], xw[:].bitcast(U32).indirect(offs_l[:]))
+        obs_b = keep.tile([P, S], U8, name="obs_b", align_bytes=64)
+        offs_b = keep.tile([P, S], U8, name="offs_b", align_bytes=64)
 
-        def cast(copy, wb, raw, m0, m1, t0, t1):
+        def move(plane, picked, queues):
+            for r in range(PACK):
+                queues[r % len(queues)].dma_start(plane[:].bitcast(I32)[r:P:QUAD, :], picked[:].bitcast(I32)[ROW_STEP * r : P : QUAD, :])
+
+        nc.vector.tensor_copy(obs_b[:], xs_obs[:].indirect(obs_l[:]))
+        nc.vector.tensor_copy(xs_offs[:].bitcast(I32), xs_obs[:].bitcast(I32))
+        move(obs_s, obs_b, (nc.sync, nc.scalar))
+        w1_raw = keep.tile([P, PACK * N], F32, name="w1_raw", tag="xs_w1", align_bytes=64)
+        nc.sync.dma_start(w1_raw[:], w1.rearrange("(p j) c -> p (j c)", j=PACK))
+        nc.vector.tensor_copy(offs_b[:], xs_offs[:].indirect(offs_l[:]))
+        move(offs_s, offs_b, (nc.sync,))
+        tau_v = tau.rearrange("(p t) j -> p t j", t=PACK)
+        tau_sb = keep.tile([P, PACK, S], F32, name="tau_sb", tag="xs_tau", align_bytes=64)
+        for t0 in (0, 2):
+            nc.sync.dma_start(tau_sb[:, t0 : t0 + 2, :], tau_v[:, t0 : t0 + 2, :])
+
+        def cast(copy, wb, raw, a, m0, m1):
             copy(
-                wb[:, t0:t1, m0:m1, :].rearrange("p t m j -> p m j t"),
-                raw[:].rearrange("p (j m t) -> p m j t", j=PACK, t=PACK)[:, m0:m1, :, t0:t1],
+                wb[:, :, m0:m1, :].rearrange("p t m j -> p m j t"),
+                raw[:].rearrange("p (j m t) -> p m j t", j=PACK, t=PACK)[:, m0:m1, :, 2 * a : 2 * a + 2],
             )
 
-        def quant_w(wb, codes, scales, t0, t1):
-            cols = slice(t0 * P, t1 * P)
+        def quant_w(wb, codes, scales, a):
+            cols = slice(2 * a * P, (2 * a + 2) * P)
             nc.vector.quantize_mx(
                 out=codes[:, cols].bitcast(FP8X4),
-                scales=scales(t0, t1),
-                in_=wb[:, t0:t1, :, :].rearrange("p t m j -> p (t m j)"),
+                scales=scales[:, cols],
+                in_=wb[:, :, :, :].rearrange("p t m j -> p (t m j)"),
             )
 
         def product(dst, codes, scales, t, x_codes, x_bytes):
@@ -92,139 +97,88 @@ def tile_picked_pinball_none_po_kernel(
             nc.tensor.matmul_mx(
                 out=dst,
                 lhsT=codes[:, cols].bitcast(FP8X4),
-                lhsT_scale=scales(t, t + 1),
+                lhsT_scale=scales[:, cols],
                 rhs=x_codes.bitcast(FP8X4),
                 rhs_scale=x_bytes,
                 start=True,
                 stop=True,
             )
 
-        w2b = keep.tile([P, PACK, P, PACK], BF16, name="w2b", align_bytes=64)
+        placed = ctx.enter_context(tc.tile_pool(name="placed", bufs=1))
+        w2b = [placed.tile([P, 2, P, PACK], BF16, name="w2b%d" % a, offset=a * 4 * S, align_bytes=64) for a in range(2)]
         w2c = keep.tile([P, N], U32, name="w2c", align_bytes=64)
-        ws = keep.tile([P, N + 2 * P], U8, name="ws", align_bytes=64)
-
-        def w2s(t0, t1):
-            return ws[:, t0 * P : t1 * P]
-
-        def w1s(t0, t1):
-            if t0 < 2:
-                return ws[PACK:P, (t0 + 1) * P : (t1 + 1) * P]
-            return ws[:, (t0 + 2) * P : (t1 + 2) * P]
-
-        w1b = keep.tile([P, PACK, P, PACK], BF16, name="w1b", tag="w1b_eg", align_bytes=64)
+        w2s = keep.tile([P, N], U8, name="w2s", align_bytes=64)
+        w1b = [keep.tile([P, 2, P, PACK], BF16, name="w1b%d" % a, align_bytes=64) for a in range(2)]
         w1c = keep.tile([P, N], U32, name="w1c", align_bytes=64)
-        cast(nc.scalar.copy, w2b, w2_raw, 0, W2_ON_SCALAR, 0, PACK)
-        cast(nc.vector.tensor_copy, w2b, w2_raw, W2_ON_SCALAR, P, 2, PACK)
-        cast(nc.vector.tensor_copy, w2b, w2_raw, W2_ON_SCALAR, P, 0, 2)
-        quant_w(w2b, w2c, w2s, 2, PACK)
-        quant_w(w2b, w2c, w2s, 0, 2)
+        w1s = keep.tile([P, N], U8, name="w1s", align_bytes=64)
+        cast(nc.scalar.copy, w2b[0], w2_raw, 0, 0, P)
+        cast(nc.scalar.copy, w2b[1], w2_raw, 1, 0, P // 4)
+        cast(nc.vector.tensor_copy, w2b[1], w2_raw, 1, P // 4, P)
+        quant_w(w2b[0], w2c, w2s, 0)
+        quant_w(w2b[1], w2c, w2s, 1)
+        obs_w = placed.tile([P, S], U32, name="obs_w", offset=0, align_bytes=64)
+        offs_w = placed.tile([P, S], U32, name="offs_w", offset=4 * S, align_bytes=64)
+        halves = ((0, HALF), (HALF, S))
+        for c0, c1 in halves:
+            nc.vector.tensor_copy(obs_w[:, c0:c1], xw[:].bitcast(U32).indirect(obs_l[:, c0 // GROUP : c1 // GROUP]))
+        nc.vector.tensor_copy(offs_w[:], xw[:].bitcast(U32).indirect(offs_l[:]))
+        cast(nc.vector.tensor_copy, w1b[0], w1_raw, 0, 0, P)
+        cast(nc.vector.tensor_copy, w1b[1], w1_raw, 1, 0, P // 2)
+        quant_w(w1b[0], w1c, w1s, 0)
+        cast(nc.vector.tensor_copy, w1b[1], w1_raw, 1, P // 2, P)
 
-        xq_s = keep.tile([P, 2 * S], U8, name="xq_s", align_bytes=64)
-        nc.vector.memset(xq_s[:].bitcast(I32), 0)
-        for r in range(PACK):
-            nc.scalar.dma_start(xq_s[:].bitcast(I32)[r:P:QUAD, :], picked[:].bitcast(I32)[ROW_STEP * r : P : QUAD, :])
-        obs_s = xq_s[:, 0:S]
-        offs_s = xq_s[:, S:]
+        window = [first_window, w2_raw]
+        eg = keep.tile([P, PACK, S], F32, name="eg")
+        diff0 = keep.tile([P, S], F32, name="diff0")
+        diff = [diff0[:], tau_sb[:, 0, :]]
 
-        tau_v = tau.rearrange("(p t) j -> p t j", t=PACK)
-        tau_sb = keep.tile([P, PACK, S], F32, name="tau_sb", tag="picked_tau", align_bytes=64)
-        for t0 in (2, 0):
-            nc.sync.dma_start(tau_sb[:, t0 : t0 + 2, :], tau_v[:, t0 : t0 + 2, :])
+        def dn(t0, t1, c0, c1):
+            if t0 < 2:
+                return diff[t0][:, c0:c1].unsqueeze(1)
+            return diff[c0 // HALF].rearrange("p (t c) -> p t c", t=2)[:, :, c0 % HALF : c0 % HALF + c1 - c0]
 
-        cast(nc.vector.tensor_copy, w1b, w1_raw, 0, P, 0, 2)
-        cast(nc.vector.tensor_copy, w1b, w1_raw, 0, P, 2, PACK)
-        for t0, t1 in ((0, 1), (1, 2), (2, PACK)):
-            quant_w(w1b, w1c, w1s, t0, t1)
-
-        on_w1 = [over_w1.tile([P, 2 * S], F32, name="on_w1_%d" % i, offset=i * 2 * S * 4) for i in range(2)]
-        window = [w2_raw, on_w1[0], on_w1[1], first_window]
-        eg = keep.tile([P, S], F32, name="eg", tag="w1b_eg", align_bytes=64)
-        dn = keep.tile([P, FUSED, S], F32, name="dn")
         td = keep.tile([P, PACK, S], F32, name="td")
         res = keep.tile([P, PACK, S], F32, name="res")
-        y_turned = keep.tile([P, S], F32, name="y_turned")
-        ident = keep.tile([P, P], F32, name="ident")
-        make_identity(nc, ident[:])
 
-        def target(t):
-            e_ps = psum.tile([P, S], F32, name="e_ps%d" % t, tag="bank%d" % t)
-            product(e_ps[:], w2c, w2s, t, obs_w[:], obs_s)
-            nc.scalar.mul(window[t][:, 0:S], e_ps[:], -1.0)
+        def target(t, c0, c1):
+            e_ps = psum.tile([P, c1 - c0], F32, name="e_ps%d_%d" % (t, c0), tag="e%d_%d" % (t % 2, c0))
+            product(e_ps[:], w2c, w2s, t, obs_w[:, c0:c1], obs_s[:, c0:c1])
+            nc.scalar.copy(window[t][:, c0:c1], e_ps[:])
 
-        def forecast(t):
-            y_ps = psum.tile([P, S], F32, name="y_ps%d" % t, tag="bank%d" % (PACK + t))
-            product(y_ps[:], w1c, w1s, t, offs_w[:], offs_s)
+        def look_up(t, c0, c1):
+            nc.scalar.activation(eg[:, t, c0:c1], window[t][:].indirect(at_l[:, c0 // GROUP : c1 // GROUP]), ACT.Copy)
+
+        def forecast(t0, t1, c0, c1):
+            y_ps = psum.tile([P, t1 - t0, c1 - c0], F32, name="y_ps%d_%d" % (t0, c0))
+            for t in range(t0, t1):
+                product(y_ps[:, t - t0, :], w1c, w1s, t, offs_w[:, c0:c1], offs_s[:, c0:c1])
             return y_ps
 
-        def turn_sum(dst, terms):
-            blocks = dst.shape[1] // P
-            for i, term in enumerate(terms):
-                for b in range(blocks):
-                    cols = slice(b * P, (b + 1) * P)
-                    first = i == 0 and b == 0
-                    final = i == len(terms) - 1 and b == blocks - 1
-                    nc.tensor.matmul(dst[:, cols], term[:, cols], ident[:], start=first, stop=final, is_transpose=True)
+        def compare(t0, t1, c0, c1, y):
+            nc.vector.tensor_tensor(dn(t0, t1, c0, c1), y, eg[:, t0:t1, c0:c1], ALU.subtract)
 
-        def weigh(c0, c1):
-            nc.vector.tensor_tensor(td[:, 0:FUSED, c0:c1], dn[:, :, c0:c1], tau_sb[:, 0:FUSED, c0:c1], ALU.mult)
+        def weigh(t0, t1, c0, c1):
+            nc.vector.tensor_tensor(td[:, t0:t1, c0:c1], dn(t0, t1, c0, c1), tau_sb[:, t0:t1, c0:c1], ALU.mult)
 
-        def compare(t):
-            nc.vector.tensor_tensor(dn[:, t, :], window[t][:].indirect(at_l[:]), td[:, t + 1, :], ALU.add)
+        def loss(t0, t1, c0, c1):
+            nc.vector.scalar_tensor_tensor(
+                res[:, t0:t1, c0:c1], dn(t0, t1, c0, c1), 0.0, td[:, t0:t1, c0:c1], ALU.max, ALU.subtract
+            )
 
-        target(TURNED)
-        for t in range(FUSED - 1):
-            target(t)
-            nc.scalar.copy(td[:, t + 1, :], forecast(t)[:])
-        target(FUSED - 1)
-        y_last = forecast(TURNED)
-        nc.scalar.copy(y_turned[:, 0:HALF], y_last[:, 0:HALF])
-        nc.scalar.copy(td[:, FUSED, :], forecast(FUSED - 1)[:])
-        nc.scalar.copy(y_turned[:, HALF:], y_last[:, HALF:])
-        nc.vector.tensor_copy(eg[:], window[TURNED][:].indirect(at_l[:]))
-        for t in range(FUSED):
-            compare(t)
-
-        tau_ps = psum.tile([P, S], F32, name="tau_ps", tag="bank4")
-        turn_sum(tau_ps[:], [tau_sb[:, TURNED, :]])
-        nc.scalar.mul(td[:, 0, :], tau_ps[:], -1.0)
         out_v = out_0.rearrange("(p t) j -> p t j", t=PACK)
-        over = keep.tile([P, S], F32, name="over")
-        under = keep.tile([P, S], F32, name="under")
-
-        def turned_plane(h):
-            cols = slice(h * HALF, (h + 1) * HALF)
-            d_ps = psum.tile([P, HALF], F32, name="d_ps%d" % h, tag="bank%d" % h)
-            turn_sum(d_ps[:], [eg[:, cols], y_turned[:, cols]])
-            nc.scalar.activation(over[:, cols], d_ps[:], ACT.Relu)
-            nc.vector.tensor_tensor(under[:, cols], d_ps[:], td[:, 0, cols], ALU.mult)
-            o_ps = psum.tile([P, HALF], F32, name="o_ps%d" % h, tag="bank%d" % (h + 2))
-            turn_sum(o_ps[:], [over[:, cols], under[:, cols]])
-            nc.scalar.copy(res[:, TURNED, cols], o_ps[:])
-
         oc = keep.tile([P, S], U32, name="oc", align_bytes=64)
         osc = keep.tile([P, S], U8, name="osc", align_bytes=64)
         words_v = out_1[0].rearrange("p c r -> p (c r)").bitcast(I32)
         rb = keep.tile([P, S, PACK], BF16, name="rb", align_bytes=64)
 
-        def loss(c0, c1):
-            nc.vector.scalar_tensor_tensor(
-                res[:, 0:FUSED, c0:c1], dn[:, :, c0:c1], 0.0, td[:, 0:FUSED, c0:c1], ALU.max, ALU.subtract
-            )
-
-        def store(c0, c1):
-            nc.sync.dma_start(out_v[:, 0:FUSED, c0:c1], res[:, 0:FUSED, c0:c1])
+        def store(t0, t1, c0, c1):
+            nc.sync.dma_start(out_v[:, t0:t1, c0:c1], res[:, t0:t1, c0:c1])
 
         def round_out(copy, c0, c1):
             copy(
                 rb[:, c0:c1, :].rearrange("p (a i) t -> p a t i", i=RUN),
                 res[:, :, c0:c1].rearrange("p t (a i) -> p a t i", i=RUN),
             )
-
-        def finish(c):
-            c0, c1 = c * QUARTER, (c + 1) * QUARTER
-            loss(c0, c1)
-            store(c0, c1)
-            round_out(nc.scalar.copy, c0, c1)
 
         def quant_out(c0, c1):
             nc.vector.quantize_mx(
@@ -237,24 +191,59 @@ def tile_picked_pinball_none_po_kernel(
             nc.sync.dma_start(words_v[:, c0:c1], oc[:, c0:c1].bitcast(I32))
 
         last = S - QUARTER
-        eighths = [(last, last + EIGHTH), (last + EIGHTH, S)]
-        turned_plane(0)
-        weigh(0, HALF)
-        turned_plane(1)
-        nc.sync.dma_start(out_v[:, TURNED, :], res[:, TURNED, :])
-        finish(0)
-        weigh(HALF, last)
-        finish(1)
-        finish(2)
-        for c0, c1 in eighths:
-            weigh(c0, c1)
-        for c0, c1 in eighths:
-            loss(c0, c1)
-        store(last, S)
-        round_out(nc.scalar.copy, *eighths[0])
+        for c0, c1 in halves:
+            for t in range(2):
+                target(t, c0, c1)
+        for t in range(2):
+            look_up(t, 0, S)
+        for t in range(2, PACK):
+            window.append(keep.tile([P, S], F32, name="e_late%d" % t, tag="window%d" % (t - 2), align_bytes=64))
+            target(t, 0, S)
+        quarters = [(c0, c0 + QUARTER) for c0 in range(0, S, QUARTER)]
+        for c0, c1 in quarters:
+            for t in range(2, PACK):
+                look_up(t, c0, c1)
+
+        y_first = forecast(0, 1, 0, S)
+        quant_w(w1b[1], w1c, w1s, 1)
+        for c0, c1 in halves:
+            compare(0, 1, c0, c1, y_first[:, :, c0:c1])
+        for c0, c1 in halves:
+            weigh(0, 1, c0, c1)
+        loss(0, 1, 0, HALF)
+        compare(1, 2, 0, S, forecast(1, 2, 0, S)[:])
+        loss(0, 1, HALF, S)
+        store(0, 1, 0, S)
+        weigh(1, 2, 0, S)
+        y_late = [forecast(2, PACK, c0, c1) for c0, c1 in halves]
+
+        def compare_late(q):
+            c0 = q % 2 * QUARTER
+            compare(2, PACK, *quarters[q], y_late[q // 2][:, :, c0 : c0 + QUARTER])
+
+        compare_late(0)
+        loss(1, 2, 0, S)
+        store(1, 2, 0, S)
+        compare_late(1)
+        weigh(2, PACK, *quarters[0])
+        compare_late(2)
+        weigh(2, PACK, *quarters[1])
+        loss(2, PACK, *quarters[0])
+        round_out(nc.scalar.copy, *quarters[0])
+        compare_late(3)
+        loss(2, PACK, *quarters[1])
+        store(2, PACK, 0, HALF)
+        round_out(nc.scalar.copy, *quarters[1])
+        weigh(2, PACK, *quarters[2])
+        weigh(2, PACK, *quarters[3])
+        loss(2, PACK, *quarters[2])
+        round_out(nc.scalar.copy, *quarters[2])
+        loss(2, PACK, *quarters[3])
+        store(2, PACK, HALF, S)
         quant_out(0, HALF)
         store_words(0, HALF)
-        round_out(nc.vector.tensor_copy, *eighths[1])
+        round_out(nc.scalar.copy, last, last + EIGHTH)
+        round_out(nc.vector.tensor_copy, last + EIGHTH, S)
         quant_out(HALF, last)
         quant_out(last, S)
         store_words(HALF, S)

@@ -84,12 +84,12 @@ def tile_picked_pinball_none_po_kernel(
                 raw[:].rearrange("p (j m t) -> p m j t", j=PACK, t=PACK)[:, m0:m1, :, 2 * a : 2 * a + 2],
             )
 
-        def quant_w(wb, codes, scales, a):
-            cols = slice(2 * a * P, (2 * a + 2) * P)
+        def quant_w(wb, codes, scales, t0, t1):
+            cols = slice(t0 * P, t1 * P)
             nc.vector.quantize_mx(
                 out=codes[:, cols].bitcast(FP8X4),
                 scales=scales[:, cols],
-                in_=wb[:, :, :, :].rearrange("p t m j -> p (t m j)"),
+                in_=wb.rearrange("p t m j -> p (t m j)"),
             )
 
         def product(dst, codes, scales, t, x_codes, x_bytes):
@@ -108,14 +108,14 @@ def tile_picked_pinball_none_po_kernel(
         w2b = [placed.tile([P, 2, P, PACK], BF16, name="w2b%d" % a, offset=a * 4 * S, align_bytes=64) for a in range(2)]
         w2c = keep.tile([P, N], U32, name="w2c", align_bytes=64)
         w2s = keep.tile([P, N], U8, name="w2s", align_bytes=64)
-        w1b = [keep.tile([P, 2, P, PACK], BF16, name="w1b%d" % a, align_bytes=64) for a in range(2)]
+        w1b = [keep.tile([P, 2, P, PACK], BF16, name="w1b%d" % a, tag="w1b%d" % a, align_bytes=64) for a in range(2)]
         w1c = keep.tile([P, N], U32, name="w1c", align_bytes=64)
         w1s = keep.tile([P, N], U8, name="w1s", align_bytes=64)
         cast(nc.scalar.copy, w2b[0], w2_raw, 0, 0, P)
         cast(nc.scalar.copy, w2b[1], w2_raw, 1, 0, P // 4)
         cast(nc.vector.tensor_copy, w2b[1], w2_raw, 1, P // 4, P)
-        quant_w(w2b[0], w2c, w2s, 0)
-        quant_w(w2b[1], w2c, w2s, 1)
+        quant_w(w2b[0][:], w2c, w2s, 0, 2)
+        quant_w(w2b[1][:], w2c, w2s, 2, PACK)
         obs_w = placed.tile([P, S], U32, name="obs_w", offset=0, align_bytes=64)
         offs_w = placed.tile([P, S], U32, name="offs_w", offset=4 * S, align_bytes=64)
         halves = ((0, HALF), (HALF, S))
@@ -124,18 +124,22 @@ def tile_picked_pinball_none_po_kernel(
         nc.vector.tensor_copy(offs_w[:], xw[:].bitcast(U32).indirect(offs_l[:]))
         cast(nc.vector.tensor_copy, w1b[0], w1_raw, 0, 0, P)
         cast(nc.vector.tensor_copy, w1b[1], w1_raw, 1, 0, P // 2)
-        quant_w(w1b[0], w1c, w1s, 0)
+        quant_w(w1b[0][:, 0:1, :, :], w1c, w1s, 0, 1)
         cast(nc.vector.tensor_copy, w1b[1], w1_raw, 1, P // 2, P)
+        quant_w(w1b[0][:, 1:2, :, :], w1c, w1s, 1, 2)
 
-        window = [first_window, w2_raw]
+        second_window = keep.tile([P, S], F32, name="second_window", tag="window1", align_bytes=64)
+        window = [first_window, second_window]
         eg = keep.tile([P, PACK, S], F32, name="eg")
         diff0 = keep.tile([P, S], F32, name="diff0")
-        diff = [diff0[:], tau_sb[:, 0, :]]
+        diff = [diff0[:]]
 
         def dn(t0, t1, c0, c1):
             if t0 < 2:
                 return diff[t0][:, c0:c1].unsqueeze(1)
-            return diff[c0 // HALF].rearrange("p (t c) -> p t c", t=2)[:, :, c0 % HALF : c0 % HALF + c1 - c0]
+            q = c0 // QUARTER
+            block = diff[q // 2][:, q % 2 * HALF : (q % 2 + 1) * HALF].rearrange("p (t c) -> p t c", t=2)
+            return block[:, :, c0 % QUARTER : c0 % QUARTER + c1 - c0]
 
         td = keep.tile([P, PACK, S], F32, name="td")
         res = keep.tile([P, PACK, S], F32, name="res")
@@ -194,8 +198,9 @@ def tile_picked_pinball_none_po_kernel(
         for c0, c1 in halves:
             for t in range(2):
                 target(t, c0, c1)
-        for t in range(2):
-            look_up(t, 0, S)
+        look_up(0, 0, S)
+        for c0, c1 in halves:
+            look_up(1, c0, c1)
         for t in range(2, PACK):
             window.append(keep.tile([P, S], F32, name="e_late%d" % t, tag="window%d" % (t - 2), align_bytes=64))
             target(t, 0, S)
@@ -204,17 +209,17 @@ def tile_picked_pinball_none_po_kernel(
             for t in range(2, PACK):
                 look_up(t, c0, c1)
 
-        y_first = forecast(0, 1, 0, S)
-        quant_w(w1b[1], w1c, w1s, 1)
+        compare(0, 1, 0, S, forecast(0, 1, 0, S)[:])
+        quant_w(w1b[1][:], w1c, w1s, 2, PACK)
+        diff1 = keep.tile([P, S], F32, name="diff1", tag="w1b1", align_bytes=64)
+        diff.append(diff1[:])
+        y_second = forecast(1, 2, 0, S)
         for c0, c1 in halves:
-            compare(0, 1, c0, c1, y_first[:, :, c0:c1])
-        for c0, c1 in halves:
-            weigh(0, 1, c0, c1)
-        loss(0, 1, 0, HALF)
-        compare(1, 2, 0, S, forecast(1, 2, 0, S)[:])
-        loss(0, 1, HALF, S)
-        store(0, 1, 0, S)
+            compare(1, 2, c0, c1, y_second[:, :, c0:c1])
+        weigh(0, 1, 0, S)
         weigh(1, 2, 0, S)
+        loss(0, 1, 0, S)
+        store(0, 1, 0, S)
         y_late = [forecast(2, PACK, c0, c1) for c0, c1 in halves]
 
         def compare_late(q):
@@ -231,20 +236,20 @@ def tile_picked_pinball_none_po_kernel(
         loss(2, PACK, *quarters[0])
         round_out(nc.scalar.copy, *quarters[0])
         compare_late(3)
+        weigh(2, PACK, *quarters[2])
         loss(2, PACK, *quarters[1])
         store(2, PACK, 0, HALF)
         round_out(nc.scalar.copy, *quarters[1])
-        weigh(2, PACK, *quarters[2])
         weigh(2, PACK, *quarters[3])
         loss(2, PACK, *quarters[2])
         round_out(nc.scalar.copy, *quarters[2])
-        loss(2, PACK, *quarters[3])
-        store(2, PACK, HALF, S)
         quant_out(0, HALF)
         store_words(0, HALF)
+        loss(2, PACK, *quarters[3])
+        store(2, PACK, HALF, S)
         round_out(nc.scalar.copy, last, last + EIGHTH)
-        round_out(nc.vector.tensor_copy, last + EIGHTH, S)
         quant_out(HALF, last)
+        round_out(nc.vector.tensor_copy, last + EIGHTH, S)
         quant_out(last, S)
         store_words(HALF, S)
         srows = out_2[0].bitcast(I32)

@@ -138,7 +138,8 @@ def tile_picked_pinball_none_po_kernel(
             if t0 < 2:
                 return diff[t0][:, c0:c1].unsqueeze(1)
             q = c0 // QUARTER
-            block = diff[q // 2][:, q % 2 * HALF : (q % 2 + 1) * HALF].rearrange("p (t c) -> p t c", t=2)
+            place = (diff[0][:, 0:HALF], diff[0][:, HALF:S], diff[1][:, 0:HALF], td[:, 1, 0:HALF])[q]
+            block = place.rearrange("p (t c) -> p t c", t=2)
             return block[:, :, c0 % QUARTER : c0 % QUARTER + c1 - c0]
 
         td = keep.tile([P, PACK, S], F32, name="td")
@@ -226,31 +227,37 @@ def tile_picked_pinball_none_po_kernel(
             c0 = q % 2 * QUARTER
             compare(2, PACK, *quarters[q], y_late[q // 2][:, :, c0 : c0 + QUARTER])
 
+        eighths = ((last, last + EIGHTH), (last + EIGHTH, S))
         compare_late(0)
-        loss(1, 2, 0, S)
-        store(1, 2, 0, S)
+        loss(1, 2, 0, last)
+        store(1, 2, 0, last)
         compare_late(1)
         weigh(2, PACK, *quarters[0])
         compare_late(2)
         weigh(2, PACK, *quarters[1])
         loss(2, PACK, *quarters[0])
+        store(2, PACK, *quarters[0])
         round_out(nc.scalar.copy, *quarters[0])
         compare_late(3)
         weigh(2, PACK, *quarters[2])
         loss(2, PACK, *quarters[1])
-        store(2, PACK, 0, HALF)
         round_out(nc.scalar.copy, *quarters[1])
-        weigh(2, PACK, *quarters[3])
+        weigh(2, PACK, *eighths[0])
         loss(2, PACK, *quarters[2])
+        store(2, PACK, QUARTER, last)
         round_out(nc.scalar.copy, *quarters[2])
+        weigh(2, PACK, *eighths[1])
+        loss(1, 2, last, S)
+        loss(2, PACK, *eighths[0])
+        round_out(nc.scalar.copy, *eighths[0])
+        loss(2, PACK, *eighths[1])
+        store(1, PACK, last, S)
         quant_out(0, HALF)
         store_words(0, HALF)
-        loss(2, PACK, *quarters[3])
-        store(2, PACK, HALF, S)
-        round_out(nc.scalar.copy, last, last + EIGHTH)
-        quant_out(HALF, last)
-        round_out(nc.vector.tensor_copy, last + EIGHTH, S)
-        quant_out(last, S)
+        round_out(nc.vector.tensor_copy, *eighths[1])
+        quant_out(*quarters[2])
+        quant_out(*eighths[0])
+        quant_out(*eighths[1])
         store_words(HALF, S)
         srows = out_2[0].bitcast(I32)
         for q in range(P // QUAD):

@@ -162,12 +162,17 @@ def tile_picked_pinball_none_po_kernel(
         def compare(t0, t1, c0, c1, y):
             nc.vector.tensor_tensor(dn(t0, t1, c0, c1), y, eg[:, t0:t1, c0:c1], ALU.subtract)
 
-        def weigh(t0, t1, c0, c1):
-            nc.vector.tensor_tensor(td[:, t0:t1, c0:c1], dn(t0, t1, c0, c1), tau_sb[:, t0:t1, c0:c1], ALU.mult)
+        def weighed(t0, t1, c0, c1):
+            if (t0, c0) == (1, S - QUARTER):
+                return td[:, 0:1, 0:QUARTER]
+            return td[:, t0:t1, c0:c1]
+
+        def weigh(t0, t1, c0, c1, engine=nc.vector):
+            engine.tensor_tensor(weighed(t0, t1, c0, c1), dn(t0, t1, c0, c1), tau_sb[:, t0:t1, c0:c1], ALU.mult)
 
         def loss(t0, t1, c0, c1):
             nc.vector.scalar_tensor_tensor(
-                res[:, t0:t1, c0:c1], dn(t0, t1, c0, c1), 0.0, td[:, t0:t1, c0:c1], ALU.max, ALU.subtract
+                res[:, t0:t1, c0:c1], dn(t0, t1, c0, c1), 0.0, weighed(t0, t1, c0, c1), ALU.max, ALU.subtract
             )
 
         out_v = out_0.rearrange("(p t) j -> p t j", t=PACK)
@@ -206,7 +211,10 @@ def tile_picked_pinball_none_po_kernel(
             window.append(keep.tile([P, S], F32, name="e_late%d" % t, tag="window%d" % (t - 2), align_bytes=64))
             target(t, 0, S)
         quarters = [(c0, c0 + QUARTER) for c0 in range(0, S, QUARTER)]
-        for c0, c1 in quarters:
+        look_up(2, 0, HALF)
+        for c0, c1 in quarters[:2]:
+            look_up(3, c0, c1)
+        for c0, c1 in quarters[2:]:
             for t in range(2, PACK):
                 look_up(t, c0, c1)
 
@@ -217,9 +225,11 @@ def tile_picked_pinball_none_po_kernel(
         y_second = forecast(1, 2, 0, S)
         for c0, c1 in halves:
             compare(1, 2, c0, c1, y_second[:, :, c0:c1])
-        weigh(0, 1, 0, S)
-        weigh(1, 2, 0, S)
+        weigh(0, 1, 0, 128, nc.gpsimd)
+        weigh(0, 1, 128, S)
+        weigh(1, 2, 0, last)
         loss(0, 1, 0, S)
+        weigh(1, 2, last, S, nc.gpsimd)
         store(0, 1, 0, S)
         y_late = [forecast(2, PACK, c0, c1) for c0, c1 in halves]
 

@@ -111,9 +111,13 @@ def tile_picked_pinball_none_po_kernel(
         w1b = [keep.tile([P, 2, P, PACK], BF16, name="w1b%d" % a, tag="w1b%d" % a, align_bytes=64) for a in range(2)]
         w1c = keep.tile([P, N], U32, name="w1c", align_bytes=64)
         w1s = keep.tile([P, N], U8, name="w1s", align_bytes=64)
-        cast(nc.scalar.copy, w2b[0], w2_raw, 0, 0, P)
-        cast(nc.scalar.copy, w2b[1], w2_raw, 1, 0, P // 4)
-        cast(nc.vector.tensor_copy, w2b[1], w2_raw, 1, P // 4, P)
+        cast(nc.scalar.copy, w2b[0], w2_raw, 0, 0, 96)
+        nc.gpsimd.tensor_copy(
+            w2b[0][:, :, 96:P, :],
+            w2_raw[:].rearrange("p (j m t) -> p t m j", j=PACK, t=PACK)[:, 0:2, 96:P, :],
+        )
+        cast(nc.scalar.copy, w2b[1], w2_raw, 1, 0, 48)
+        cast(nc.vector.tensor_copy, w2b[1], w2_raw, 1, 48, P)
         quant_w(w2b[0][:], w2c, w2s, 0, 2)
         quant_w(w2b[1][:], w2c, w2s, 2, PACK)
         obs_w = placed.tile([P, S], U32, name="obs_w", offset=0, align_bytes=64)
@@ -225,8 +229,8 @@ def tile_picked_pinball_none_po_kernel(
         y_second = forecast(1, 2, 0, S)
         for c0, c1 in halves:
             compare(1, 2, c0, c1, y_second[:, :, c0:c1])
-        weigh(0, 1, 0, 128, nc.gpsimd)
-        weigh(0, 1, 128, S)
+        weigh(0, 1, 0, 176, nc.gpsimd)
+        weigh(0, 1, 176, S)
         weigh(1, 2, 0, last)
         loss(0, 1, 0, S)
         weigh(1, 2, last, S, nc.gpsimd)
@@ -248,14 +252,14 @@ def tile_picked_pinball_none_po_kernel(
         loss(2, PACK, *quarters[0])
         store(2, PACK, *quarters[0])
         round_out(nc.scalar.copy, *quarters[0])
-        compare_late(3)
         weigh(2, PACK, *quarters[2])
         loss(2, PACK, *quarters[1])
         round_out(nc.scalar.copy, *quarters[1])
-        weigh(2, PACK, *eighths[0])
+        compare_late(3)
         loss(2, PACK, *quarters[2])
         store(2, PACK, QUARTER, last)
         round_out(nc.scalar.copy, *quarters[2])
+        weigh(2, PACK, *eighths[0])
         weigh(2, PACK, *eighths[1])
         loss(1, 2, last, S)
         loss(2, PACK, *eighths[0])

@@ -111,13 +111,13 @@ def tile_picked_pinball_none_po_kernel(
         w1b = [keep.tile([P, 2, P, PACK], BF16, name="w1b%d" % a, tag="w1b%d" % a, align_bytes=64) for a in range(2)]
         w1c = keep.tile([P, N], U32, name="w1c", align_bytes=64)
         w1s = keep.tile([P, N], U8, name="w1s", align_bytes=64)
-        cast(nc.scalar.copy, w2b[0], w2_raw, 0, 0, 96)
+        cast(nc.scalar.copy, w2b[0], w2_raw, 0, 0, 88)
         nc.gpsimd.tensor_copy(
-            w2b[0][:, :, 96:P, :],
-            w2_raw[:].rearrange("p (j m t) -> p t m j", j=PACK, t=PACK)[:, 0:2, 96:P, :],
+            w2b[0][:, :, 88:P, :],
+            w2_raw[:].rearrange("p (j m t) -> p t m j", j=PACK, t=PACK)[:, 0:2, 88:P, :],
         )
-        cast(nc.scalar.copy, w2b[1], w2_raw, 1, 0, 48)
-        cast(nc.vector.tensor_copy, w2b[1], w2_raw, 1, 48, P)
+        cast(nc.scalar.copy, w2b[1], w2_raw, 1, 0, 64)
+        cast(nc.vector.tensor_copy, w2b[1], w2_raw, 1, 64, P)
         quant_w(w2b[0][:], w2c, w2s, 0, 2)
         quant_w(w2b[1][:], w2c, w2s, 2, PACK)
         obs_w = placed.tile([P, S], U32, name="obs_w", offset=0, align_bytes=64)
@@ -141,8 +141,9 @@ def tile_picked_pinball_none_po_kernel(
         def dn(t0, t1, c0, c1):
             if t0 < 2:
                 return diff[t0][:, c0:c1].unsqueeze(1)
-            q = c0 // QUARTER
-            place = (diff[0][:, 0:HALF], diff[0][:, HALF:S], diff[1][:, 0:HALF], td[:, 1, 0:HALF])[q]
+            if c0 < HALF:
+                return diff[0].rearrange("p (t c) -> p t c", t=2)[:, t0 - 2 : t1 - 2, c0:c1]
+            place = diff[1][:, 0:HALF] if c0 < S - QUARTER else td[:, 1, 0:HALF]
             block = place.rearrange("p (t c) -> p t c", t=2)
             return block[:, :, c0 % QUARTER : c0 % QUARTER + c1 - c0]
 
@@ -215,9 +216,8 @@ def tile_picked_pinball_none_po_kernel(
             window.append(keep.tile([P, S], F32, name="e_late%d" % t, tag="window%d" % (t - 2), align_bytes=64))
             target(t, 0, S)
         quarters = [(c0, c0 + QUARTER) for c0 in range(0, S, QUARTER)]
-        look_up(2, 0, HALF)
-        for c0, c1 in quarters[:2]:
-            look_up(3, c0, c1)
+        for t in range(2, PACK):
+            look_up(t, 0, HALF)
         for c0, c1 in quarters[2:]:
             for t in range(2, PACK):
                 look_up(t, c0, c1)
@@ -229,8 +229,8 @@ def tile_picked_pinball_none_po_kernel(
         y_second = forecast(1, 2, 0, S)
         for c0, c1 in halves:
             compare(1, 2, c0, c1, y_second[:, :, c0:c1])
-        weigh(0, 1, 0, 176, nc.gpsimd)
-        weigh(0, 1, 176, S)
+        weigh(0, 1, 0, 304, nc.gpsimd)
+        weigh(0, 1, 304, S)
         weigh(1, 2, 0, last)
         loss(0, 1, 0, S)
         weigh(1, 2, last, S, nc.gpsimd)
@@ -242,13 +242,13 @@ def tile_picked_pinball_none_po_kernel(
             compare(2, PACK, *quarters[q], y_late[q // 2][:, :, c0 : c0 + QUARTER])
 
         eighths = ((last, last + EIGHTH), (last + EIGHTH, S))
-        compare_late(0)
         loss(1, 2, 0, last)
         store(1, 2, 0, last)
-        compare_late(1)
-        weigh(2, PACK, *quarters[0])
+        for t in range(2, PACK):
+            compare(t, t + 1, 0, HALF, y_late[0][:, t - 2 : t - 1, :])
+        for t in range(2, PACK):
+            weigh(t, t + 1, 0, HALF)
         compare_late(2)
-        weigh(2, PACK, *quarters[1])
         loss(2, PACK, *quarters[0])
         store(2, PACK, *quarters[0])
         round_out(nc.scalar.copy, *quarters[0])

@@ -111,13 +111,13 @@ def tile_picked_pinball_none_po_kernel(
         w1b = [keep.tile([P, 2, P, PACK], BF16, name="w1b%d" % a, tag="w1b%d" % a, align_bytes=64) for a in range(2)]
         w1c = keep.tile([P, N], U32, name="w1c", align_bytes=64)
         w1s = keep.tile([P, N], U8, name="w1s", align_bytes=64)
-        cast(nc.scalar.copy, w2b[0], w2_raw, 0, 0, 88)
+        cast(nc.scalar.copy, w2b[0], w2_raw, 0, 0, 96)
         nc.gpsimd.tensor_copy(
-            w2b[0][:, :, 88:P, :],
-            w2_raw[:].rearrange("p (j m t) -> p t m j", j=PACK, t=PACK)[:, 0:2, 88:P, :],
+            w2b[0][:, :, 96:P, :],
+            w2_raw[:].rearrange("p (j m t) -> p t m j", j=PACK, t=PACK)[:, 0:2, 96:P, :],
         )
-        cast(nc.scalar.copy, w2b[1], w2_raw, 1, 0, 64)
-        cast(nc.vector.tensor_copy, w2b[1], w2_raw, 1, 64, P)
+        cast(nc.scalar.copy, w2b[1], w2_raw, 1, 0, 48)
+        cast(nc.vector.tensor_copy, w2b[1], w2_raw, 1, 48, P)
         quant_w(w2b[0][:], w2c, w2s, 0, 2)
         quant_w(w2b[1][:], w2c, w2s, 2, PACK)
         obs_w = placed.tile([P, S], U32, name="obs_w", offset=0, align_bytes=64)
@@ -229,8 +229,8 @@ def tile_picked_pinball_none_po_kernel(
         y_second = forecast(1, 2, 0, S)
         for c0, c1 in halves:
             compare(1, 2, c0, c1, y_second[:, :, c0:c1])
-        weigh(0, 1, 0, 304, nc.gpsimd)
-        weigh(0, 1, 304, S)
+        weigh(0, 1, 0, 144, nc.gpsimd)
+        weigh(0, 1, 144, S)
         weigh(1, 2, 0, last)
         loss(0, 1, 0, S)
         weigh(1, 2, last, S, nc.gpsimd)

@@ -229,8 +229,8 @@ def tile_picked_pinball_none_po_kernel(
         y_second = forecast(1, 2, 0, S)
         for c0, c1 in halves:
             compare(1, 2, c0, c1, y_second[:, :, c0:c1])
-        weigh(0, 1, 0, 144, nc.gpsimd)
-        weigh(0, 1, 144, S)
+        weigh(0, 1, 0, 192, nc.gpsimd)
+        weigh(0, 1, 192, S)
         weigh(1, 2, 0, last)
         loss(0, 1, 0, S)
         weigh(1, 2, last, S, nc.gpsimd)
@@ -246,8 +246,9 @@ def tile_picked_pinball_none_po_kernel(
         store(1, 2, 0, last)
         for t in range(2, PACK):
             compare(t, t + 1, 0, HALF, y_late[0][:, t - 2 : t - 1, :])
-        for t in range(2, PACK):
-            weigh(t, t + 1, 0, HALF)
+        weigh(2, 3, 0, HALF)
+        weigh(3, PACK, 0, 176)
+        weigh(3, PACK, 176, HALF, nc.gpsimd)
         compare_late(2)
         loss(2, PACK, *quarters[0])
         store(2, PACK, *quarters[0])

from contextlib import ExitStack

import concourse.mybir as mybir

K, T, S, N = 512, 2048, 512, 512
FLOPS = 2 * 2 * K * N * S

F32 = mybir.dt.float32
BF16 = mybir.dt.bfloat16
I32 = mybir.dt.int32
U32 = mybir.dt.uint32
U16 = mybir.dt.uint16
U8 = mybir.dt.uint8
FP8X4 = mybir.dt.float8_e4m3fn_x4
ALU = mybir.AluOpType
ACT = mybir.ActivationFunctionType

P = 128
PACK = 4
QUAD = 32
GROUP = 16
ROW_STEP = 8
HALF = 256
QUARTER = 128
EIGHTH = 64
RUN = 4


def tile_picked_pinball_none_po_kernel(
    tc, x_words, x_scales, w1, w2, tau, offs, obs, at, out_0, out_1, out_2
):
    nc = tc.nc
    with ExitStack() as ctx:
        keep = ctx.enter_context(tc.tile_pool(name="keep", bufs=1))
        psum = ctx.enter_context(tc.psum_pool(name="psum", bufs=1))

        obs_l = keep.tile([P, S // GROUP], U16, name="obs_l")
        offs_l = keep.tile([P, S // GROUP], U16, name="offs_l")
        at_l = keep.tile([P, S // GROUP], U16, name="at_l")
        xs_obs = keep.tile([P, T], U8, name="xs_obs", tag="xs_w1", align_bytes=64)
        xs_offs = keep.tile([P, T], U8, name="xs_offs", tag="xs_tau", align_bytes=64)
        xw = keep.tile([P, T], I32, name="xw", align_bytes=64)
        w2_raw = keep.tile([P, PACK * N], F32, name="w2_raw", tag="window1", align_bytes=64)
        w2_v = w2.rearrange("(p j) c -> p (j c)", j=PACK)
        obs_s = keep.tile([P, S], U8, name="obs_s", align_bytes=64)
        offs_s = keep.tile([P, S], U8, name="offs_s", align_bytes=64)
        for plane in (xs_obs, obs_s, offs_s):
            nc.vector.memset(plane[:].bitcast(I32), 0)
        nc.sync.dma_start(w2_raw[:, 0:N], w2_v[:, 0:N])
        nc.sync.dma_start(obs_l[:], obs)
        nc.sync.dma_start(offs_l[:], offs)
        nc.sync.dma_start(xs_obs[:].bitcast(I32)[0:P:ROW_STEP, :], x_scales[0].bitcast(I32))
        nc.sync.dma_start(w2_raw[:, N:], w2_v[:, N:])
        nc.sync.dma_start(xw[:], x_words[0].rearrange("p c r -> p (c r)").bitcast(I32))
        nc.sync.dma_start(at_l[:], at)

        zero = keep.tile([P, 8], F32, name="zero")
        nc.vector.memset(zero[:], 0.0)
        first_window = keep.tile([P, 2 * S], F32, name="first_window", tag="window0", align_bytes=64)
        nc.scalar.mul(first_window[:, S:], zero[:, 0:1].to_broadcast([P, S]), 1.0)

        obs_b = keep.tile([P, S], U8, name="obs_b", align_bytes=64)
        offs_b = keep.tile([P, S], U8, name="offs_b", align_bytes=64)

        def move(plane, picked, queues):
            for r in range(PACK):
                queues[r % len(queues)].dma_start(plane[:].bitcast(I32)[r:P:QUAD, :], picked[:].bitcast(I32)[ROW_STEP * r : P : QUAD, :])

        nc.vector.tensor_copy(obs_b[:], xs_obs[:].indirect(obs_l[:]))
        nc.vector.tensor_copy(xs_offs[:].bitcast(I32), xs_obs[:].bitcast(I32))
        move(obs_s, obs_b, (nc.sync, nc.scalar))
        w1_raw = keep.tile([P, PACK * N], F32, name="w1_raw", tag="xs_w1", align_bytes=64)
        nc.sync.dma_start(w1_raw[:], w1.rearrange("(p j) c -> p (j c)", j=PACK))
        nc.vector.tensor_copy(offs_b[:], xs_offs[:].indirect(offs_l[:]))
        move(offs_s, offs_b, (nc.sync,))
        tau_v = tau.rearrange("(p t) j -> p t j", t=PACK)
        tau_sb = keep.tile([P, PACK, S], F32, name="tau_sb", tag="xs_tau", align_bytes=64)
        for t0 in (0, 2):
            nc.sync.dma_start(tau_sb[:, t0 : t0 + 2, :], tau_v[:, t0 : t0 + 2, :])

        def cast(copy, wb, raw, a, m0, m1):
            copy(
                wb[:, :, m0:m1, :].rearrange("p t m j -> p m j t"),
                raw[:].rearrange("p (j m t) -> p m j t", j=PACK, t=PACK)[:, m0:m1, :, 2 * a : 2 * a + 2],
            )

        def quant_w(wb, codes, scales, t0, t1):
            cols = slice(t0 * P, t1 * P)
            nc.vector.quantize_mx(
                out=codes[:, cols].bitcast(FP8X4),
                scales=scales[:, cols],
                in_=wb.rearrange("p t m j -> p (t m j)"),
            )

        def product(dst, codes, scales, t, x_codes, x_bytes):
            cols = slice(t * P, (t + 1) * P)
            nc.tensor.matmul_mx(
                out=dst,
                lhsT=codes[:, cols].bitcast(FP8X4),
                lhsT_scale=scales[:, cols],
                rhs=x_codes.bitcast(FP8X4),
                rhs_scale=x_bytes,
                start=True,
                stop=True,
            )

        placed = ctx.enter_context(tc.tile_pool(name="placed", bufs=1))
        w2b = [placed.tile([P, 2, P, PACK], BF16, name="w2b%d" % a, offset=a * 4 * S, align_bytes=64) for a in range(2)]
        w2c = keep.tile([P, N], U32, name="w2c", align_bytes=64)
        w2s = keep.tile([P, N], U8, name="w2s", align_bytes=64)
        w1b = [keep.tile([P, 2, P, PACK], BF16, name="w1b%d" % a, tag="w1b%d" % a, align_bytes=64) for a in range(2)]
        w1c = keep.tile([P, N], U32, name="w1c", align_bytes=64)
        w1s = keep.tile([P, N], U8, name="w1s", align_bytes=64)
        cast(nc.scalar.copy, w2b[0], w2_raw, 0, 0, 96)
        nc.gpsimd.tensor_copy(
            w2b[0][:, :, 96:P, :],
            w2_raw[:].rearrange("p (j m t) -> p t m j", j=PACK, t=PACK)[:, 0:2, 96:P, :],
        )
        cast(nc.scalar.copy, w2b[1], w2_raw, 1, 0, 48)
        cast(nc.vector.tensor_copy, w2b[1], w2_raw, 1, 48, P)
        quant_w(w2b[0][:], w2c, w2s, 0, 2)
        quant_w(w2b[1][:], w2c, w2s, 2, PACK)
        obs_w = placed.tile([P, S], U32, name="obs_w", offset=0, align_bytes=64)
        offs_w = placed.tile([P, S], U32, name="offs_w", offset=4 * S, align_bytes=64)
        halves = ((0, HALF), (HALF, S))
        for c0, c1 in halves:
            nc.vector.tensor_copy(obs_w[:, c0:c1], xw[:].bitcast(U32).indirect(obs_l[:, c0 // GROUP : c1 // GROUP]))
        nc.vector.tensor_copy(offs_w[:], xw[:].bitcast(U32).indirect(offs_l[:]))
        cast(nc.vector.tensor_copy, w1b[0], w1_raw, 0, 0, P)
        cast(nc.vector.tensor_copy, w1b[1], w1_raw, 1, 0, P // 2)
        quant_w(w1b[0][:, 0:1, :, :], w1c, w1s, 0, 1)
        cast(nc.vector.tensor_copy, w1b[1], w1_raw, 1, P // 2, P)
        quant_w(w1b[0][:, 1:2, :, :], w1c, w1s, 1, 2)

        second_window = keep.tile([P, S], F32, name="second_window", tag="window1", align_bytes=64)
        window = [first_window, second_window]
        eg = keep.tile([P, PACK, S], F32, name="eg")
        diff0 = keep.tile([P, S], F32, name="diff0")
        diff = [diff0[:]]

        def dn(t0, t1, c0, c1):
            if t0 < 2:
                return diff[t0][:, c0:c1].unsqueeze(1)
            if c0 < HALF:
                return diff[0].rearrange("p (t c) -> p t c", t=2)[:, t0 - 2 : t1 - 2, c0:c1]
            place = diff[1][:, 0:HALF] if c0 < S - QUARTER else td[:, 1, 0:HALF]
            block = place.rearrange("p (t c) -> p t c", t=2)
            return block[:, :, c0 % QUARTER : c0 % QUARTER + c1 - c0]

        td = keep.tile([P, PACK, S], F32, name="td")
        res = keep.tile([P, PACK, S], F32, name="res")

        def target(t, c0, c1):
            e_ps = psum.tile([P, c1 - c0], F32, name="e_ps%d_%d" % (t, c0), tag="e%d_%d" % (t % 2, c0))
            product(e_ps[:], w2c, w2s, t, obs_w[:, c0:c1], obs_s[:, c0:c1])
            nc.scalar.copy(window[t][:, c0:c1], e_ps[:])

        def look_up(t, c0, c1):
            nc.scalar.activation(eg[:, t, c0:c1], window[t][:].indirect(at_l[:, c0 // GROUP : c1 // GROUP]), ACT.Copy)

        def forecast(t0, t1, c0, c1):
            y_ps = psum.tile([P, t1 - t0, c1 - c0], F32, name="y_ps%d_%d" % (t0, c0))
            for t in range(t0, t1):
                product(y_ps[:, t - t0, :], w1c, w1s, t, offs_w[:, c0:c1], offs_s[:, c0:c1])
            return y_ps

        def compare(t0, t1, c0, c1, y):
            nc.vector.tensor_tensor(dn(t0, t1, c0, c1), y, eg[:, t0:t1, c0:c1], ALU.subtract)

        def weighed(t0, t1, c0, c1):
            if (t0, c0) == (1, S - QUARTER):
                return td[:, 0:1, 0:QUARTER]
            return td[:, t0:t1, c0:c1]

        def weigh(t0, t1, c0, c1, engine=nc.vector):
            engine.tensor_tensor(weighed(t0, t1, c0, c1), dn(t0, t1, c0, c1), tau_sb[:, t0:t1, c0:c1], ALU.mult)

        def loss(t0, t1, c0, c1):
            nc.vector.scalar_tensor_tensor(
                res[:, t0:t1, c0:c1], dn(t0, t1, c0, c1), 0.0, weighed(t0, t1, c0, c1), ALU.max, ALU.subtract
            )

        out_v = out_0.rearrange("(p t) j -> p t j", t=PACK)
        oc = keep.tile([P, S], U32, name="oc", align_bytes=64)
        osc = keep.tile([P, S], U8, name="osc", align_bytes=64)
        words_v = out_1[0].rearrange("p c r -> p (c r)").bitcast(I32)
        rb = keep.tile([P, S, PACK], BF16, name="rb", align_bytes=64)

        def store(t0, t1, c0, c1):
            nc.sync.dma_start(out_v[:, t0:t1, c0:c1], res[:, t0:t1, c0:c1])

        def round_out(copy, c0, c1):
            copy(
                rb[:, c0:c1, :].rearrange("p (a i) t -> p a t i", i=RUN),
                res[:, :, c0:c1].rearrange("p t (a i) -> p a t i", i=RUN),
            )

        def quant_out(c0, c1):
            nc.vector.quantize_mx(
                out=oc[:, c0:c1].bitcast(FP8X4),
                scales=osc[:, c0:c1],
                in_=rb[:, c0:c1, :].rearrange("p a t -> p (a t)"),
            )

        def store_words(c0, c1):
            nc.sync.dma_start(words_v[:, c0:c1], oc[:, c0:c1].bitcast(I32))

        last = S - QUARTER
        for c0, c1 in halves:
            for t in range(2):
                target(t, c0, c1)
        look_up(0, 0, S)
        for c0, c1 in halves:
            look_up(1, c0, c1)
        for t in range(2, PACK):
            window.append(keep.tile([P, S], F32, name="e_late%d" % t, tag="window%d" % (t - 2), align_bytes=64))
            target(t, 0, S)
        quarters = [(c0, c0 + QUARTER) for c0 in range(0, S, QUARTER)]
        for t in range(2, PACK):
            look_up(t, 0, HALF)
        for c0, c1 in quarters[2:]:
            for t in range(2, PACK):
                look_up(t, c0, c1)

        compare(0, 1, 0, S, forecast(0, 1, 0, S)[:])
        quant_w(w1b[1][:], w1c, w1s, 2, PACK)
        diff1 = keep.tile([P, S], F32, name="diff1", tag="w1b1", align_bytes=64)
        diff.append(diff1[:])
        y_second = forecast(1, 2, 0, S)
        for c0, c1 in halves:
            compare(1, 2, c0, c1, y_second[:, :, c0:c1])
        weigh(0, 1, 0, 192, nc.gpsimd)
        weigh(0, 1, 192, S)
        weigh(1, 2, 0, last)
        loss(0, 1, 0, S)
        weigh(1, 2, last, S, nc.gpsimd)
        store(0, 1, 0, S)
        y_late = [forecast(2, PACK, c0, c1) for c0, c1 in halves]

        def compare_late(q):
            c0 = q % 2 * QUARTER
            compare(2, PACK, *quarters[q], y_late[q // 2][:, :, c0 : c0 + QUARTER])

        eighths = ((last, last + EIGHTH), (last + EIGHTH, S))
        loss(1, 2, 0, last)
        store(1, 2, 0, last)
        for t in range(2, PACK):
            compare(t, t + 1, 0, HALF, y_late[0][:, t - 2 : t - 1, :])
        weigh(2, 3, 0, HALF)
        weigh(3, PACK, 0, 176)
        weigh(3, PACK, 176, HALF, nc.gpsimd)
        compare_late(2)
        loss(2, PACK, *quarters[0])
        store(2, PACK, *quarters[0])
        round_out(nc.scalar.copy, *quarters[0])
        weigh(2, PACK, *quarters[2])
        loss(2, PACK, *quarters[1])
        round_out(nc.scalar.copy, *quarters[1])
        compare_late(3)
        loss(2, PACK, *quarters[2])
        store(2, PACK, QUARTER, last)
        round_out(nc.scalar.copy, *quarters[2])
        weigh(2, PACK, *eighths[0])
        weigh(2, PACK, *eighths[1])
        loss(1, 2, last, S)
        loss(2, PACK, *eighths[0])
        round_out(nc.scalar.copy, *eighths[0])
        loss(2, PACK, *eighths[1])
        store(1, PACK, last, S)
        quant_out(0, HALF)
        store_words(0, HALF)
        round_out(nc.vector.tensor_copy, *eighths[1])
        quant_out(*quarters[2])
        quant_out(*eighths[0])
        quant_out(*eighths[1])
        store_words(HALF, S)
        srows = out_2[0].bitcast(I32)
        for q in range(P // QUAD):
            queue = nc.scalar if q % 2 else nc.sync
            queue.dma_start(srows[PACK * q : PACK * (q + 1), :], osc[:].bitcast(I32)[QUAD * q : QUAD * q + PACK, :])
